import numpy as np
import ml_dtypes


def mxq(x, axis, fmt="e4m3"):
    dtype, down = {"e4m3": (ml_dtypes.float8_e4m3fn, 7), "e5m2": (ml_dtypes.float8_e5m2, 14)}[fmt]
    v = np.moveaxis(np.asarray(x, np.float32).astype(ml_dtypes.bfloat16).astype(np.float64), axis, -1)
    blocks = v.reshape(v.shape[:-1] + (-1, 32))
    amax = np.abs(blocks).max(-1, keepdims=True)
    byte = np.maximum(np.where(amax > 0, np.frexp(amax)[1] - 1 + 127, 0) - down, 1)
    scale = np.exp2(byte - 127.0)
    codes = (blocks / scale).astype(np.float32).astype(dtype).astype(np.float64)
    return np.moveaxis((codes * scale).reshape(v.shape), -1, axis)


WIDE = False


def mx_kscale(k):
    if not WIDE:
        return np.ones(k)
    levels = np.array([10, -10, 5, -5, 0])
    if k % 512:
        return np.exp2(np.random.permutation(np.resize(levels, k // 32))).repeat(32)
    a = np.empty((k // 512, 16))
    for p in range(k // 512):
        a[p, :8] = np.random.permutation(np.resize(levels, 8))
        for g in range(8):
            far = levels[np.abs(levels - a[p, g]) >= 10]
            a[p, g + 8] = far[np.random.randint(len(far))]
    return np.exp2(a.ravel()).repeat(32)


BF16 = ml_dtypes.bfloat16


def bf(x):
    return np.asarray(x, np.float32).astype(BF16)


def f64(x):
    return np.asarray(x).astype(np.float64)


E2M1 = np.array([0.0, 0.5, 1.0, 1.5, 2.0, 3.0, 4.0, 6.0, -0.0, -0.5, -1.0, -1.5, -2.0, -3.0, -4.0, -6.0])


def pack_weight(w, fmt):
    k, n = w.shape
    w = f64(bf(w)).reshape(k // 32, 32, n)
    amax = np.abs(w).max(1)
    if fmt == "e4m3":
        byte = np.frexp(amax)[1] - 1 + 127 - 7
    else:
        mant, ex = np.frexp(amax / 6.0)
        byte = np.where(mant > 0.5, ex, ex - 1) + 127
    byte = np.clip(np.where(amax > 0, byte, 1), 1, 254)
    scaled = (w * np.exp2(127.0 - byte)[:, None, :]).reshape(k, n).astype(np.float32)
    by_word = np.ascontiguousarray(scaled.reshape(k // 512, 128, 4, n).transpose(0, 1, 3, 2))
    if fmt == "e4m3":
        words = by_word.astype(ml_dtypes.float8_e4m3fn).view(np.uint8)
    else:
        c = by_word.astype(ml_dtypes.float4_e2m1fn).view(np.uint8) & 0xF
        words = c[..., 0::2] | (c[..., 1::2] << 4)
    return np.ascontiguousarray(words), np.ascontiguousarray(byte.astype(np.uint8).reshape(k // 512, 16, n))


def unpack_weight(words, scales, fmt):
    g, p, n, _ = words.shape
    if fmt == "e4m3":
        vals = np.ascontiguousarray(words).view(ml_dtypes.float8_e4m3fn).astype(np.float64)
    else:
        nib = np.empty((g, p, n, 4), np.uint8)
        nib[..., 0::2] = words & 0xF
        nib[..., 1::2] = words >> 4
        vals = E2M1[nib]
    vals = vals * np.repeat(np.exp2(scales.astype(np.float64) - 127.0), 8, axis=1)[..., None]
    return vals.transpose(0, 1, 3, 2).reshape(g * 512, n)
def pack4(w):
    words, scales = pack_weight(w, "e2m1")
    return words.reshape(words.shape[0], 128, -1), scales


def unpack4(words, scales):
    return unpack_weight(words.reshape(words.shape[0], 128, -1, 2), scales, "e2m1")


def planes(Y):
    n, m = Y.shape
    b = f64(bf(Y)).reshape(n // 32, 32, m)
    amax = np.abs(b).max(1)
    byte = np.clip(np.where(amax > 0, np.frexp(amax)[1] - 1 + 127 - 7, 1), 1, 254)
    codes = (b * np.exp2(127.0 - byte)[:, None, :]).reshape(n, m).astype(np.float32).astype(ml_dtypes.float8_e4m3fn).view(np.uint8)
    words = codes.reshape(n // 512, 128, 4, m).transpose(0, 1, 3, 2)
    return np.ascontiguousarray(words), np.ascontiguousarray(byte.astype(np.uint8).reshape(n // 512, 16, m))


N, M, S, D, C = 1024, 512, 512, 512, 3
Q = (C + 1) * M


def hermite_kernel(x, cen):
    v = x[:, None, :] - cen[None, :, :]
    r2 = np.sum(v * v, axis=-1)
    psi = np.exp(-r2 / 4.0)
    blocks = [psi]
    for c in range(x.shape[1]):
        blocks.append(0.5 * v[:, :, c] * psi)
    return np.concatenate(blocks, axis=1)


def setup_inputs():
    s, t = mx_kscale(D), mx_kscale(Q)
    x = bf(np.random.standard_normal((N, C)))
    cen = bf(np.random.standard_normal((M, C)))
    z = bf(np.random.standard_normal((S, D)) * s)
    a_words, a_scales = pack4(np.random.standard_normal((D, Q)) / np.sqrt(D) / s[:, None] / t[None, :])
    return {
        "x": x,
        "cen": cen,
        "z": z,
        "a_words": a_words,
        "a_scales": a_scales,
        "b": bf(0.5 * np.random.standard_normal(Q) / t),
        "q": bf(12.0 / np.sqrt(Q) * np.random.standard_normal(Q) * t),
    }


def core(x, cen, z, a_words, a_scales, b, q):
    ker = hermite_kernel(f64(x), f64(cen))
    kq = ker * f64(q)[None, :]
    w = (mxq(f64(z), 1, "e4m3") @ unpack4(a_words, a_scales)) + f64(b)[None, :]
    return mxq(kq, 1, "e4m3") @ mxq(w, 1, "e4m3").T


def reference(x, cen, z, a_words, a_scales, b, q):
    R_out = core(x, cen, z, a_words, a_scales, b, q)
    words, scales = planes(R_out)
    return R_out, words, scales

@@ -1,0 +1,414 @@
+from contextlib import ExitStack
+
+import concourse.mybir as mybir
+from concourse.masks import make_identity
+
+F32 = mybir.dt.float32
+BF16 = mybir.dt.bfloat16
+I32 = mybir.dt.int32
+U32 = mybir.dt.uint32
+U8 = mybir.dt.uint8
+FP8X4 = mybir.dt.float8_e4m3fn_x4
+FP4X4 = mybir.dt.float4_e2m1fn_x4
+ACTF = mybir.ActivationFunctionType
+ALU = mybir.AluOpType
+
+P = 128
+N, M, S, D, C = 1024, 512, 512, 512, 3
+G = C + 1
+NT = N // P
+FLOPS = 2 * S * D * G * M + 2 * N * S * G * M
+
+
+def fours(ap):
+    return ap.rearrange("p (a i) t -> p a t i", i=4)
+
+
+def slots(ap):
+    return ap.rearrange("p t (a i) -> p a t i", i=4)
+
+
+def tile_hermitegaussianrbfimplicitshapespace_x2_kernel(
+    tc, x, cen, z, a_words, a_scales, b, q, out_0, out_1, out_2
+):
+    nc = tc.nc
+    with ExitStack() as ctx:
+        keep = ctx.enter_context(tc.tile_pool(name="keep", bufs=1))
+        work = ctx.enter_context(tc.tile_pool(name="work", bufs=3))
+        psum = ctx.enter_context(tc.psum_pool(name="psum", bufs=2))
+
+        ctx.enter_context(tc.manual_schedule())
+
+        vrow = keep.tile([P, 512], BF16, align_bytes=64)
+        xn = keep.tile([P, NT, C], BF16, align_bytes=64)
+        z_sb = keep.tile([P, 4, D], BF16, align_bytes=64)
+        a_raw = keep.tile([P, 4096], U8, align_bytes=64)
+        as_raw = keep.tile([P, 2048], U8, align_bytes=64)
+        nc.vector.memset(vrow[:].bitcast(I32), 0)
+        nc.gpsimd.memset(as_raw[:].bitcast(I32), 0)
+        nc.scalar.dma_start(
+            out=xn[:].rearrange("p (g t) c -> p g (t c)", g=2),
+            in_=x.rearrange("(g p t) c -> p g (t c)", g=2, t=4),
+        )
+        z_rows = z.rearrange("(u p) d -> p u d", p=P)
+        nc.sync.dma_start(out=z_sb[:, 0:2, :], in_=z_rows[:, 0:2, :])
+        nc.sync.dma_start(out=z_sb[:, 2:4, :], in_=z_rows[:, 2:4, :])
+        nc.scalar.dma_start(
+            out=vrow[8:12, 0:384].rearrange("j (b x) -> j b x", x=24),
+            in_=cen.rearrange("(b j i) c -> j b (i c)", j=4, i=8),
+        )
+        nc.scalar.dma_start(
+            out=vrow[0:4, :].rearrange("t (a i) -> t a i", i=8),
+            in_=q.rearrange("(a t i) -> t a i", t=4, i=8),
+        )
+        nc.scalar.dma_start(
+            out=vrow[4:8, :].rearrange("t (a i) -> t a i", i=8),
+            in_=b.rearrange("(a t i) -> t a i", t=4, i=8),
+        )
+        for h in range(2):
+            cols = slice(2048 * h, 2048 * h + 2048)
+            nc.sync.dma_start(out=a_raw[:, cols].bitcast(I32), in_=a_words[0][:, cols].bitcast(I32))
+        for Q in range(4):
+            nc.scalar.dma_start(
+                out=as_raw[32 * Q : 32 * Q + 4, :].bitcast(I32),
+                in_=a_scales[0][4 * Q : 4 * Q + 4, :].bitcast(I32),
+            )
+        ident = keep.tile([P, P], BF16, align_bytes=64)
+        make_identity(nc, ident[:])
+        ident32 = keep.tile([P, P], F32, align_bytes=64)
+        make_identity(nc, ident32[:])
+
+        warm = keep.tile([P, 1], F32)
+        nc.vector.memset(warm[:], 0.0)
+        nc.scalar.activation(out=warm[:], in_=warm[:], func=ACTF.Exp)
+        xf = keep.tile([P, NT, P], BF16, align_bytes=64)
+        nc.vector.memset(xf[:].bitcast(I32), 0)
+        nc.vector.memset(xf[:, :, 16:22], 1.0)
+        sf = keep.tile([P, 8, P], BF16, align_bytes=64)
+        nc.vector.memset(sf[:].bitcast(I32), 0)
+        nc.vector.memset(sf[:, 0:4, 32:38], -0.25)
+        nc.vector.tensor_copy(out=xf[:, :, 0:3], in_=xn[:])
+        x2 = keep.tile([P, NT, C], F32)
+        nc.vector.tensor_tensor(out=x2[:], in0=xn[:], in1=xn[:], op=ALU.mult)
+        nc.vector.tensor_copy(out=xf[:, :, 32:35], in_=x2[:])
+        nc.vector.tensor_tensor(out=xf[:, :, 35:38], in0=x2[:], in1=xf[:, :, 32:35], op=ALU.subtract)
+
+        zw = z_sb[:].rearrange("p u d -> p (u d)").bitcast(F32)
+        zg = keep.tile([P, S, 4], BF16, align_bytes=64)
+        zgw = zg[:].rearrange("p s t -> p (s t)").bitcast(F32).rearrange("p (h v s u) -> p h v s u", h=2, v=2, u=2)
+
+        def turn_z(h, copy):
+            z_ps = psum.tile([P, 2, 2, P], F32, tag="p")
+            for v in range(2):
+                base = 256 * (2 * h + v)
+                for u in range(2):
+                    nc.tensor.transpose(z_ps[:, v, u, :], zw[:, base + u : base + 256 : 2], ident32[:])
+            copy(out=zgw[:, h], in_=z_ps[:].rearrange("p v u s -> p v s u"))
+
+        turn_z(0, nc.vector.tensor_copy)
+        xt_ps = psum.tile([P, NT, P], BF16, tag="e")
+        for nt in range(NT):
+            nc.tensor.transpose(xt_ps[:, nt, :], xf[:, nt, :], ident[:])
+        xt = keep.tile([P, NT, P], BF16, align_bytes=64)
+        nc.scalar.copy(out=xt[:], in_=xt_ps[:])
+        turn_z(1, nc.scalar.copy)
+
+        v_ps = psum.tile([P, 7, P], BF16, tag="w")
+        for g in range(G):
+            nc.tensor.transpose(v_ps[:, g, :], vrow[:, P * g : P * g + P], ident[:])
+        for c in range(C):
+            nc.tensor.transpose(v_ps[:, 4 + c, :], vrow[:, c : 384 : 3], ident[:])
+        vv = keep.tile([P, 7, 12], F32)
+        nc.vector.tensor_copy(out=vv[:], in_=v_ps[:, :, 0:12])
+        cv = vv[:, 4:7, 8:12]
+        cvj = cv.rearrange("p c j -> p j c")
+
+        hq = keep.tile([P, C, 4], F32)
+        nc.vector.tensor_scalar_mul(out=hq[:], in0=vv[:, 1:4, 0:4], scalar1=0.5)
+        kn = keep.tile([P, C, 4], F32)
+        nc.vector.scalar_tensor_tensor(out=kn[:], in0=hq[:], scalar=-1.0, in1=cv, op0=ALU.mult, op1=ALU.mult)
+        nc.vector.tensor_scalar_mul(out=sf[:, 0:4, 0:3], in0=cvj, scalar1=0.5)
+        c2 = keep.tile([P, 4, C], F32)
+        nc.vector.scalar_tensor_tensor(out=c2[:], in0=cvj, scalar=-0.25, in1=cvj, op0=ALU.mult, op1=ALU.mult)
+        nc.vector.tensor_copy(out=sf[:, 0:4, 16:19], in_=c2[:])
+        nc.vector.tensor_tensor(out=sf[:, 0:4, 19:22], in0=c2[:], in1=sf[:, 0:4, 16:19], op=ALU.subtract)
+        nc.vector.tensor_copy(out=sf[:, 4:8, 0], in_=hq[:, 0, :])
+        nc.vector.tensor_copy(out=sf[:, 4:8, 16], in_=kn[:, 0, :])
+        nc.vector.tensor_tensor(out=sf[:, 4:8, 19], in0=kn[:, 0, :], in1=sf[:, 4:8, 16], op=ALU.subtract)
+
+        a_sb = keep.tile([P, 4096], U8, align_bytes=64)
+        as_sb = keep.tile([P, 2048], U8, align_bytes=64)
+
+        def order_a(g, eng):
+            for dst, raw, w in ((a_sb, a_raw, 4), (as_sb, as_raw, 2)):
+                n = 64 * w
+                eng.tensor_copy(
+                    out=dst[:].bitcast(I32)[:, g * n : g * n + n].rearrange("p (t b w) -> p t b w", t=4, w=w),
+                    in_=raw[:].bitcast(I32)[:, g * n : g * n + n].rearrange("p (b t w) -> p t b w", t=4, w=w),
+                )
+
+        order_a(0, nc.vector)
+        zc = keep.tile([P, S], U32, align_bytes=64)
+        zs = keep.tile([P, S], U8, align_bytes=64)
+        nc.vector.quantize_mx(out=zc[:].bitcast(FP8X4), scales=zs[:], in_=zg[:].rearrange("p s t -> p (s t)"))
+
+        order_a(1, nc.gpsimd)
+        order_a(3, nc.gpsimd)
+
+        st_ps = psum.tile([P, 8, P], BF16, tag="e")
+        for k in range(8):
+            nc.tensor.transpose(st_ps[:, k, :], sf[:, k, :], ident[:])
+        sT = keep.tile([P, 8, P], BF16, align_bytes=64)
+        nc.scalar.copy(out=sT[:], in_=st_ps[:])
+
+        psi = keep.tile([P, 4, N], F32, align_bytes=64)
+
+        def make_psi(nt):
+            e_ps = psum.tile([P, 4, P], F32, tag="e")
+            for j in range(4):
+                nc.tensor.matmul(e_ps[:, j, :], lhsT=sT[:, j, :], rhs=xt[:, nt, :], start=True, stop=True)
+            nc.scalar.activation(out=psi[:, :, P * nt : P * nt + P], in_=e_ps[:], func=ACTF.Exp)
+
+        pc = keep.tile([P, 2, 4, N], F32, align_bytes=64)
+        xb = keep.tile([P, 2, N], BF16, align_bytes=64)
+
+        def spread_points(c):
+            xb_ps = psum.tile([P, N], BF16, tag="o")
+            for nt in range(NT):
+                nc.tensor.transpose(xb_ps[:, P * nt : P * nt + P], xn[:, nt, c : c + 1].to_broadcast([P, P]), ident[:])
+            nc.scalar.copy(out=xb[:, c - 1, :], in_=xb_ps[:])
+
+        def make_slopes(c, h):
+            cols = slice(512 * h, 512 * h + 512)
+            for j in range(4):
+                nc.gpsimd.tensor_scalar(
+                    out=pc[:, c - 1, j, cols], in0=xb[:, c - 1, cols],
+                    scalar1=hq[:, c, j : j + 1], scalar2=kn[:, c, j : j + 1], op0=ALU.mult, op1=ALU.add,
+                )
+
+        wc = keep.tile([P, G, S], U32, align_bytes=64)
+        ws = keep.tile([P, G, S], U8, align_bytes=64)
+
+        def w_matmul(out, k, cols):
+            nc.tensor.matmul_mx(
+                out=out,
+                lhsT=a_sb[:, 256 * k : 256 * k + 256].bitcast(FP4X4),
+                lhsT_scale=as_sb[:, P * k : P * k + P],
+                rhs=zc[:, cols].bitcast(FP8X4),
+                rhs_scale=zs[:, cols],
+                start=True,
+                stop=True,
+            )
+
+        def w_quarter(g, u, wb):
+            w_ps = psum.tile([P, 4, P], F32, tag="w")
+            cols = slice(P * u, P * u + P)
+            for t in range(4):
+                w_matmul(w_ps[:, t, :], 4 * g + t, cols)
+            nc.vector.tensor_tensor(
+                out=wb[:, cols, :],
+                in0=w_ps[:].rearrange("p t s -> p s t"),
+                in1=vv[:, g : g + 1, 4:8].to_broadcast([P, P, 4]),
+                op=ALU.add,
+            )
+
+        def w_quant(g, wb):
+            nc.vector.quantize_mx(
+                out=wc[:, g, :].bitcast(FP8X4), scales=ws[:, g, :], in_=wb[:].rearrange("p s t -> p (s t)")
+            )
+
+        w3 = keep.tile([P, 4, S], BF16, align_bytes=64)
+
+        def w_slot(g, t, tag):
+            w_ps = psum.tile([P, S], F32, tag=tag)
+            w_matmul(w_ps[:], 4 * g + t, slice(0, S))
+            nc.scalar.activation(out=w3[:, t, :], in_=w_ps[:], func=ACTF.Identity, bias=vv[:, g, 4 + t : 5 + t], scale=1.0)
+
+        def w_join(h, wb):
+            cols = slice(256 * h, 256 * h + 256)
+            nc.scalar.copy(out=fours(wb[:, cols, :]), in_=slots(w3[:, :, cols]))
+
+        wbs = [work.tile([P, S, 4], BF16, align_bytes=64, bufs=4, name="wb") for g in range(G)]
+        extra = {
+            0: lambda: (spread_points(1), spread_points(2), order_a(2, nc.gpsimd), make_slopes(1, 0), make_slopes(2, 0)),
+            1: lambda: make_psi(0),
+            2: lambda: (w_slot(3, 0, "p"), w_slot(3, 1, "p")),
+            3: lambda: make_psi(1),
+            4: lambda: (w_slot(3, 2, "o"), w_slot(3, 3, "o"), make_slopes(1, 1), make_slopes(2, 1)),
+            5: lambda: make_psi(2),
+            6: lambda: w_join(0, wbs[3]),
+            7: lambda: (make_psi(3), w_join(1, wbs[3])),
+            8: lambda: make_psi(4),
+        }
+        for g in range(3):
+            for u in range(4):
+                w_quarter(g, u, wbs[g])
+                if g > 0 and u == 0:
+                    w_quant(g - 1, wbs[g - 1])
+                if 4 * g + u in extra:
+                    extra[4 * g + u]()
+
+        kc = keep.tile([P, NT // 2, G, 2 * P], U32, align_bytes=64)
+        ks = keep.tile([P, NT // 2, G, 2 * P], U8, align_bytes=64)
+        of = keep.tile([P, 2, 4, S], F32, align_bytes=64)
+        out_rows = out_0.rearrange("(g p t) m -> g t p m", g=2, t=4)
+
+        def scaled_psi(n0, n1):
+            kq0 = work.tile([P, 4, 2 * P], BF16, align_bytes=64, bufs=3)
+            for j in range(4):
+                nc.scalar.activation(
+                    out=kq0[:, j, 0 : P * (n1 - n0)],
+                    in_=psi[:, j, P * n0 : P * n1],
+                    func=ACTF.Copy,
+                    scale=vv[:, 0, j : j + 1],
+                )
+            return kq0
+
+        def first_block(n0, n1, kq0, kb):
+            nc.scalar.copy(out=fours(kb[:, 0, 0 : P * (n1 - n0), :]), in_=slots(kq0[:, :, 0 : P * (n1 - n0)]))
+
+        slope = {}
+
+        def slopes_0(n0, n1):
+            for nt in range(n0, n1):
+                p_ps = psum.tile([P, 4, P], F32, tag="p")
+                slope[nt] = p_ps
+                for j in range(4):
+                    nc.tensor.matmul(p_ps[:, j, :], lhsT=sT[:, 4 + j, :], rhs=xt[:, nt, :], start=True, stop=True)
+
+        def second_block(n0, n1, kb):
+            for nt in range(n0, n1):
+                nc.vector.tensor_tensor(
+                    out=fours(kb[:, 1, P * (nt - n0) : P * (nt - n0) + P, :]),
+                    in0=slots(slope[nt][:]),
+                    in1=slots(psi[:, :, P * nt : P * nt + P]),
+                    op=ALU.mult,
+                )
+
+        def other_block(n0, n1, c, kb):
+            nc.vector.tensor_tensor(
+                out=fours(kb[:, 2 + c, 0 : (n1 - n0) * P, :]),
+                in0=slots(pc[:, c, :, P * n0 : P * n1]),
+                in1=slots(psi[:, :, P * n0 : P * n1]),
+                op=ALU.mult,
+            )
+
+        def quant_pair(n0, kb):
+            nc.vector.quantize_mx(
+                out=kc[:, n0 // 2].rearrange("p g n -> p (g n)").bitcast(FP8X4),
+                scales=ks[:, n0 // 2].rearrange("p g n -> p (g n)"),
+                in_=kb[:].rearrange("p g n t -> p (g n t)"),
+            )
+
+        def quant_block(nt, g, kb):
+            off = P * (nt % 2)
+            nc.vector.quantize_mx(
+                out=kc[:, nt // 2, g, off : off + P].bitcast(FP8X4),
+                scales=ks[:, nt // 2, g, off : off + P],
+                in_=kb[:, g, 0:P, :].rearrange("p n t -> p (n t)"),
+            )
+
+        def stage2_pass(o_ap, nt, g, cols, first, last):
+            off = P * (nt % 2)
+            nc.tensor.matmul_mx(
+                out=o_ap,
+                lhsT=kc[:, nt // 2, g, off : off + P].bitcast(FP8X4),
+                lhsT_scale=ks[:, nt // 2, g, off : off + P],
+                rhs=wc[:, g, cols].bitcast(FP8X4),
+                rhs_scale=ws[:, g, cols],
+                start=first,
+                stop=last,
+            )
+
+        def stage2(nt):
+            o_ps = psum.tile([P, S], F32, tag="o")
+            for g in range(G):
+                stage2_pass(o_ps[:], nt, g, slice(0, S), g == 0, g == G - 1)
+            nc.scalar.copy(out=of[:, nt // 4, nt % 4, :], in_=o_ps[:])
+            nc.sync.dma_start(out=out_rows[nt // 4, nt % 4], in_=of[:, nt // 4, nt % 4, :])
+
+        o_bf = [keep.tile([P, S, 4], BF16, align_bytes=64, name="ob%d" % h) for h in range(2)]
+        ocs = [keep.tile([P, S], U32, align_bytes=64, name="oc%d" % h) for h in range(2)]
+        oss = [keep.tile([P, S], U8, align_bytes=64, name="osc%d" % h) for h in range(2)]
+
+        def join_out(h, copy, cols):
+            copy(out=fours(o_bf[h][:, cols, :]), in_=slots(of[:, h, :, cols]))
+
+        def quant_out(h, cols):
+            nc.vector.quantize_mx(
+                out=ocs[h][:, cols].bitcast(FP8X4), scales=oss[h][:, cols], in_=o_bf[h][:, cols, :].rearrange("p m t -> p (m t)")
+            )
+            nc.sync.dma_start(
+                out=out_1[h][:, cols, :].rearrange("p m t -> p (m t)").bitcast(I32), in_=ocs[h][:, cols].bitcast(I32)
+            )
+
+        def store_scales(h):
+            for Q in range(4):
+                nc.sync.dma_start(
+                    out=out_2[h][4 * Q : 4 * Q + 4, :].bitcast(I32),
+                    in_=oss[h][32 * Q : 32 * Q + 4, :].bitcast(I32),
+                )
+
+        groups = [(0, 2), (2, 4), (4, 6), (6, 7), (7, 8)]
+        later_psi = {0: [5, 6], 1: [7]}
+        kbs = [work.tile([P, G, 2 * P, 4], BF16, align_bytes=64, bufs=5, name="kb") for i in groups]
+
+        def first(i):
+            first_block(*groups[i], scaled_psi(*groups[i]), kbs[i])
+
+        first(0)
+        slopes_0(0, 2)
+        for i in range(3):
+            n0, n1 = groups[i]
+            second_block(n0, n1, kbs[i])
+            slopes_0(*groups[i + 1])
+            if i == 0:
+                w_quant(2, wbs[2])
+                w_quant(3, wbs[3])
+            else:
+                quant_pair(groups[i - 1][0], kbs[i - 1])
+            for nt in later_psi.get(i, ()):
+                make_psi(nt)
+            first(i + 1)
+            for c in range(2):
+                other_block(n0, n1, c, kbs[i])
+            if i > 0:
+                for nt in range(*groups[i - 1]):
+                    stage2(nt)
+        second_block(6, 7, kbs[3])
+        slopes_0(7, 8)
+        quant_pair(4, kbs[2])
+        first(4)
+        other_block(6, 7, 0, kbs[3])
+        stage2(4)
+        stage2(5)
+        quant_block(6, 0, kbs[3])
+        quant_block(6, 1, kbs[3])
+        other_block(6, 7, 1, kbs[3])
+        quant_block(6, 2, kbs[3])
+        second_block(7, 8, kbs[4])
+        quant_block(6, 3, kbs[3])
+        join_out(0, nc.scalar.copy, slice(0, S))
+        stage2(6)
+        other_block(7, 8, 0, kbs[4])
+        quant_block(7, 0, kbs[4])
+        quant_block(7, 1, kbs[4])
+        other_block(7, 8, 1, kbs[4])
+        quant_block(7, 2, kbs[4])
+        quant_block(7, 3, kbs[4])
+        ends = [psum.tile([P, S // 2], F32, tag="p", name="o_end") for h in range(2)]
+        for g in range(G):
+            for h in range(2):
+                stage2_pass(ends[h][:], 7, g, slice(256 * h, 256 * h + 256), g == 0, g == G - 1)
+        quant_out(0, slice(0, S))
+        store_scales(0)
+        for h, copy in ((0, nc.vector.tensor_copy), (1, nc.scalar.copy)):
+            cols = slice(256 * h, 256 * h + 256)
+            copy(out=of[:, 1, 3, cols], in_=ends[h][:])
+            nc.sync.dma_start(out=out_rows[1, 3][:, cols], in_=of[:, 1, 3, cols])
+        join_out(1, nc.vector.tensor_copy, slice(0, 256))
+        join_out(1, nc.scalar.copy, slice(384, S))
+        join_out(1, nc.vector.tensor_copy, slice(256, 384))
+        quant_out(1, slice(0, 256))
+        quant_out(1, slice(256, S))
+        store_scales(1)

@@ -39,7 +39,7 @@ def tile_hermitegaussianrbfimplicitshapespace_x2_kernel(
 
         ctx.enter_context(tc.manual_schedule())
 
-        vrow = keep.tile([P, 512], BF16, align_bytes=64)
+        vrow = keep.tile([P, 896], BF16, align_bytes=64)
         xn = keep.tile([P, NT, C], BF16, align_bytes=64)
         z_sb = keep.tile([P, 4, D], BF16, align_bytes=64)
         a_raw = keep.tile([P, 4096], U8, align_bytes=64)
@@ -52,19 +52,13 @@ def tile_hermitegaussianrbfimplicitshapespace_x2_kernel(
         )
         z_rows = z.rearrange("(u p) d -> p u d", p=P)
         nc.sync.dma_start(out=z_sb[:, 0:2, :], in_=z_rows[:, 0:2, :])
-        nc.sync.dma_start(out=z_sb[:, 2:4, :], in_=z_rows[:, 2:4, :])
+        nc.scalar.dma_start(out=vrow[0:4, 0:512], in_=q.rearrange("(g m) -> g m", g=4))
+        nc.scalar.dma_start(out=vrow[4:8, 0:512], in_=b.rearrange("(g m) -> g m", g=4))
         nc.scalar.dma_start(
-            out=vrow[8:12, 0:384].rearrange("j (b x) -> j b x", x=24),
+            out=vrow[0:4, 512:896].rearrange("j (b x) -> j b x", x=24),
             in_=cen.rearrange("(b j i) c -> j b (i c)", j=4, i=8),
         )
-        nc.scalar.dma_start(
-            out=vrow[0:4, :].rearrange("t (a i) -> t a i", i=8),
-            in_=q.rearrange("(a t i) -> t a i", t=4, i=8),
-        )
-        nc.scalar.dma_start(
-            out=vrow[4:8, :].rearrange("t (a i) -> t a i", i=8),
-            in_=b.rearrange("(a t i) -> t a i", t=4, i=8),
-        )
+        nc.sync.dma_start(out=z_sb[:, 2:4, :], in_=z_rows[:, 2:4, :])
         for h in range(2):
             cols = slice(2048 * h, 2048 * h + 2048)
             nc.sync.dma_start(out=a_raw[:, cols].bitcast(I32), in_=a_words[0][:, cols].bitcast(I32))
@@ -79,7 +73,7 @@ def tile_hermitegaussianrbfimplicitshapespace_x2_kernel(
         make_identity(nc, ident32[:])
 
         warm = keep.tile([P, 1], F32)
-        nc.vector.memset(warm[:], 0.0)
+        nc.gpsimd.memset(warm[:], 0.0)
         nc.scalar.activation(out=warm[:], in_=warm[:], func=ACTF.Exp)
         xf = keep.tile([P, NT, P], BF16, align_bytes=64)
         nc.vector.memset(xf[:].bitcast(I32), 0)
@@ -92,6 +86,26 @@ def tile_hermitegaussianrbfimplicitshapespace_x2_kernel(
         nc.vector.tensor_tensor(out=x2[:], in0=xn[:], in1=xn[:], op=ALU.mult)
         nc.vector.tensor_copy(out=xf[:, :, 32:35], in_=x2[:])
         nc.vector.tensor_tensor(out=xf[:, :, 35:38], in0=x2[:], in1=xf[:, :, 32:35], op=ALU.subtract)
+
+        vord = keep.tile([P, 4, P], BF16, align_bytes=64)
+        nc.vector.tensor_copy(
+            out=vord[:].rearrange("p t (b i) -> p t b i", i=8),
+            in_=vrow[:, 0:512].rearrange("p (b t i) -> p t b i", t=4, i=8),
+        )
+        xt_ps = psum.tile([P, NT, P], BF16, tag="e")
+        for nt in range(NT):
+            nc.tensor.transpose(xt_ps[:, nt, :], xf[:, nt, :], ident[:])
+        xt = keep.tile([P, NT, P], BF16, align_bytes=64)
+        nc.scalar.copy(out=xt[:], in_=xt_ps[:])
+        v_ps = psum.tile([P, 7, P], BF16, tag="w")
+        for t in range(4):
+            nc.tensor.transpose(v_ps[:, t, :], vord[:, t, :], ident[:])
+        for c in range(C):
+            nc.tensor.transpose(v_ps[:, 4 + c, :], vrow[:, 512 + c : 896 : 3], ident[:])
+        vv = keep.tile([P, 8, 7], F32)
+        nc.vector.tensor_copy(out=vv[:], in_=v_ps[:, :, 0:8].rearrange("p k r -> p r k"))
+        cvj = vv[:, 0:4, 4:7]
+        cv = cvj.rearrange("p j c -> p c j")
 
         zw = z_sb[:].rearrange("p u d -> p (u d)").bitcast(F32)
         zg = keep.tile([P, S, 4], BF16, align_bytes=64)
@@ -106,22 +120,7 @@ def tile_hermitegaussianrbfimplicitshapespace_x2_kernel(
             copy(out=zgw[:, h], in_=z_ps[:].rearrange("p v u s -> p v s u"))
 
         turn_z(0, nc.vector.tensor_copy)
-        xt_ps = psum.tile([P, NT, P], BF16, tag="e")
-        for nt in range(NT):
-            nc.tensor.transpose(xt_ps[:, nt, :], xf[:, nt, :], ident[:])
-        xt = keep.tile([P, NT, P], BF16, align_bytes=64)
-        nc.scalar.copy(out=xt[:], in_=xt_ps[:])
         turn_z(1, nc.scalar.copy)
-
-        v_ps = psum.tile([P, 7, P], BF16, tag="w")
-        for g in range(G):
-            nc.tensor.transpose(v_ps[:, g, :], vrow[:, P * g : P * g + P], ident[:])
-        for c in range(C):
-            nc.tensor.transpose(v_ps[:, 4 + c, :], vrow[:, c : 384 : 3], ident[:])
-        vv = keep.tile([P, 7, 12], F32)
-        nc.vector.tensor_copy(out=vv[:], in_=v_ps[:, :, 0:12])
-        cv = vv[:, 4:7, 8:12]
-        cvj = cv.rearrange("p c j -> p j c")
 
         hq = keep.tile([P, C, 4], F32)
         nc.vector.tensor_scalar_mul(out=hq[:], in0=vv[:, 1:4, 0:4], scalar1=0.5)
@@ -152,8 +151,6 @@ def tile_hermitegaussianrbfimplicitshapespace_x2_kernel(
         zs = keep.tile([P, S], U8, align_bytes=64)
         nc.vector.quantize_mx(out=zc[:].bitcast(FP8X4), scales=zs[:], in_=zg[:].rearrange("p s t -> p (s t)"))
 
-        order_a(1, nc.gpsimd)
-        order_a(3, nc.gpsimd)
 
         st_ps = psum.tile([P, 8, P], BF16, tag="e")
         for k in range(8):
@@ -170,20 +167,20 @@ def tile_hermitegaussianrbfimplicitshapespace_x2_kernel(
             nc.scalar.activation(out=psi[:, :, P * nt : P * nt + P], in_=e_ps[:], func=ACTF.Exp)
 
         pc = keep.tile([P, 2, 4, N], F32, align_bytes=64)
-        xb = keep.tile([P, 2, N], BF16, align_bytes=64)
+        spread = {}
 
         def spread_points(c):
-            xb_ps = psum.tile([P, N], BF16, tag="o")
+            spread[c] = psum.tile([P, N], BF16, tag="o", name="xb_ps")
             for nt in range(NT):
-                nc.tensor.transpose(xb_ps[:, P * nt : P * nt + P], xn[:, nt, c : c + 1].to_broadcast([P, P]), ident[:])
-            nc.scalar.copy(out=xb[:, c - 1, :], in_=xb_ps[:])
+                nc.tensor.transpose(
+                    spread[c][:, P * nt : P * nt + P], xn[:, nt, c : c + 1].to_broadcast([P, P]), ident[:]
+                )
 
-        def make_slopes(c, h):
-            cols = slice(512 * h, 512 * h + 512)
+        def make_slopes(c):
             for j in range(4):
-                nc.gpsimd.tensor_scalar(
-                    out=pc[:, c - 1, j, cols], in0=xb[:, c - 1, cols],
-                    scalar1=hq[:, c, j : j + 1], scalar2=kn[:, c, j : j + 1], op0=ALU.mult, op1=ALU.add,
+                nc.scalar.activation(
+                    out=pc[:, c - 1, j, :], in_=spread[c][:], func=ACTF.Identity,
+                    bias=kn[:, c, j : j + 1], scale=hq[:, c, j : j + 1],
                 )
 
         wc = keep.tile([P, G, S], U32, align_bytes=64)
@@ -208,7 +205,7 @@ def tile_hermitegaussianrbfimplicitshapespace_x2_kernel(
             nc.vector.tensor_tensor(
                 out=wb[:, cols, :],
                 in0=w_ps[:].rearrange("p t s -> p s t"),
-                in1=vv[:, g : g + 1, 4:8].to_broadcast([P, P, 4]),
+                in1=vv[:, 4 + g : 5 + g, 0:4].to_broadcast([P, P, 4]),
                 op=ALU.add,
             )
 
@@ -217,30 +214,17 @@ def tile_hermitegaussianrbfimplicitshapespace_x2_kernel(
                 out=wc[:, g, :].bitcast(FP8X4), scales=ws[:, g, :], in_=wb[:].rearrange("p s t -> p (s t)")
             )
 
-        w3 = keep.tile([P, 4, S], BF16, align_bytes=64)
-
-        def w_slot(g, t, tag):
-            w_ps = psum.tile([P, S], F32, tag=tag)
-            w_matmul(w_ps[:], 4 * g + t, slice(0, S))
-            nc.scalar.activation(out=w3[:, t, :], in_=w_ps[:], func=ACTF.Identity, bias=vv[:, g, 4 + t : 5 + t], scale=1.0)
-
-        def w_join(h, wb):
-            cols = slice(256 * h, 256 * h + 256)
-            nc.scalar.copy(out=fours(wb[:, cols, :]), in_=slots(w3[:, :, cols]))
-
         wbs = [work.tile([P, S, 4], BF16, align_bytes=64, bufs=4, name="wb") for g in range(G)]
         extra = {
-            0: lambda: (spread_points(1), spread_points(2), order_a(2, nc.gpsimd), make_slopes(1, 0), make_slopes(2, 0)),
-            1: lambda: make_psi(0),
-            2: lambda: (w_slot(3, 0, "p"), w_slot(3, 1, "p")),
-            3: lambda: make_psi(1),
-            4: lambda: (w_slot(3, 2, "o"), w_slot(3, 3, "o"), make_slopes(1, 1), make_slopes(2, 1)),
+            0: lambda: (order_a(1, nc.vector), make_psi(0)),
+            1: lambda: (spread_points(1), order_a(2, nc.vector), make_psi(1)),
+            2: lambda: (make_slopes(1), order_a(3, nc.vector)),
+            3: lambda: spread_points(2),
             5: lambda: make_psi(2),
-            6: lambda: w_join(0, wbs[3]),
-            7: lambda: (make_psi(3), w_join(1, wbs[3])),
-            8: lambda: make_psi(4),
+            6: lambda: make_slopes(2),
+            7: lambda: make_psi(3),
         }
-        for g in range(3):
+        for g in range(4):
             for u in range(4):
                 w_quarter(g, u, wbs[g])
                 if g > 0 and u == 0:
@@ -350,7 +334,7 @@ def tile_hermitegaussianrbfimplicitshapespace_x2_kernel(
                 )
 
         groups = [(0, 2), (2, 4), (4, 6), (6, 7), (7, 8)]
-        later_psi = {0: [5, 6], 1: [7]}
+        later_psi = {0: [4, 5], 1: [6, 7]}
         kbs = [work.tile([P, G, 2 * P, 4], BF16, align_bytes=64, bufs=5, name="kb") for i in groups]
 
         def first(i):
@@ -363,7 +347,6 @@ def tile_hermitegaussianrbfimplicitshapespace_x2_kernel(
             second_block(n0, n1, kbs[i])
             slopes_0(*groups[i + 1])
             if i == 0:
-                w_quant(2, wbs[2])
                 w_quant(3, wbs[3])
             else:
                 quant_pair(groups[i - 1][0], kbs[i - 1])

@@ -75,13 +75,20 @@ def tile_hermitegaussianrbfimplicitshapespace_x2_kernel(
         warm = keep.tile([P, 1], F32)
         nc.gpsimd.memset(warm[:], 0.0)
         nc.scalar.activation(out=warm[:], in_=warm[:], func=ACTF.Exp)
+        vzero = keep.tile([P, 512], BF16, align_bytes=64)
+        nc.vector.memset(vzero[:].bitcast(I32), 0)
+        sums = keep.tile([P, 2, 4, C], F32)
+        nc.vector.memset(sums[:], 0.0)
         xf = keep.tile([P, NT, P], BF16, align_bytes=64)
         nc.vector.memset(xf[:].bitcast(I32), 0)
         nc.vector.memset(xf[:, :, 16:22], 1.0)
         sf = keep.tile([P, 8, P], BF16, align_bytes=64)
         nc.vector.memset(sf[:].bitcast(I32), 0)
         nc.vector.memset(sf[:, 0:4, 32:38], -0.25)
-        nc.vector.tensor_copy(out=xf[:, :, 0:3], in_=xn[:])
+        chill = psum.tile([P, 512], F32, tag="o")
+        for k in range(3):
+            nc.tensor.matmul(chill[:], lhsT=vzero[:, 0:P], rhs=vzero[:], start=True, stop=True)
+        nc.scalar.copy(out=xf[:, :, 0:3], in_=xn[:])
         x2 = keep.tile([P, NT, C], F32)
         nc.vector.tensor_tensor(out=x2[:], in0=xn[:], in1=xn[:], op=ALU.mult)
         nc.vector.tensor_copy(out=xf[:, :, 32:35], in_=x2[:])
@@ -92,16 +99,16 @@ def tile_hermitegaussianrbfimplicitshapespace_x2_kernel(
             out=vord[:].rearrange("p t (b i) -> p t b i", i=8),
             in_=vrow[:, 0:512].rearrange("p (b t i) -> p t b i", t=4, i=8),
         )
+        v_ps = psum.tile([P, 7, P], BF16, tag="w")
+        for c in range(C):
+            nc.tensor.transpose(v_ps[:, 4 + c, :], vrow[:, 512 + c : 896 : 3], ident[:])
+        for t in range(4):
+            nc.tensor.transpose(v_ps[:, t, :], vord[:, t, :], ident[:])
         xt_ps = psum.tile([P, NT, P], BF16, tag="e")
         for nt in range(NT):
             nc.tensor.transpose(xt_ps[:, nt, :], xf[:, nt, :], ident[:])
         xt = keep.tile([P, NT, P], BF16, align_bytes=64)
         nc.scalar.copy(out=xt[:], in_=xt_ps[:])
-        v_ps = psum.tile([P, 7, P], BF16, tag="w")
-        for t in range(4):
-            nc.tensor.transpose(v_ps[:, t, :], vord[:, t, :], ident[:])
-        for c in range(C):
-            nc.tensor.transpose(v_ps[:, 4 + c, :], vrow[:, 512 + c : 896 : 3], ident[:])
         vv = keep.tile([P, 8, 7], F32)
         nc.vector.tensor_copy(out=vv[:], in_=v_ps[:, :, 0:8].rearrange("p k r -> p r k"))
         cvj = vv[:, 0:4, 4:7]
@@ -119,21 +126,31 @@ def tile_hermitegaussianrbfimplicitshapespace_x2_kernel(
                     nc.tensor.transpose(z_ps[:, v, u, :], zw[:, base + u : base + 256 : 2], ident32[:])
             copy(out=zgw[:, h], in_=z_ps[:].rearrange("p v u s -> p v s u"))
 
-        turn_z(0, nc.vector.tensor_copy)
-        turn_z(1, nc.scalar.copy)
-
         hq = keep.tile([P, C, 4], F32)
-        nc.vector.tensor_scalar_mul(out=hq[:], in0=vv[:, 1:4, 0:4], scalar1=0.5)
+        nc.vector.scalar_tensor_tensor(
+            out=sums[:, 0], in0=cvj, scalar=-0.25, in1=cvj, op0=ALU.mult, op1=ALU.mult
+        )
+        nc.vector.scalar_tensor_tensor(
+            out=sums[:, 1, :, 0], in0=vv[:, 1, 0:4], scalar=-0.5, in1=cv[:, 0, :], op0=ALU.mult, op1=ALU.mult
+        )
+        nc.scalar.mul(out=sf[:, 0:4, 0:3], in_=cvj, mul=0.5)
+        nc.scalar.mul(out=sf[:, 4:8, 0], in_=vv[:, 1, 0:4], mul=0.5)
+        high = sf[:, :, 16:19]
+        sums_rows = sums[:].rearrange("p e j c -> p (e j) c")
+        nc.vector.tensor_copy(out=high, in_=sums_rows)
+        nc.vector.tensor_tensor(out=sf[:, :, 19:22], in0=sums_rows, in1=high, op=ALU.subtract)
+        nc.scalar.mul(out=hq[:], in_=vv[:, 1:4, 0:4], mul=0.5)
         kn = keep.tile([P, C, 4], F32)
-        nc.vector.scalar_tensor_tensor(out=kn[:], in0=hq[:], scalar=-1.0, in1=cv, op0=ALU.mult, op1=ALU.mult)
-        nc.vector.tensor_scalar_mul(out=sf[:, 0:4, 0:3], in0=cvj, scalar1=0.5)
-        c2 = keep.tile([P, 4, C], F32)
-        nc.vector.scalar_tensor_tensor(out=c2[:], in0=cvj, scalar=-0.25, in1=cvj, op0=ALU.mult, op1=ALU.mult)
-        nc.vector.tensor_copy(out=sf[:, 0:4, 16:19], in_=c2[:])
-        nc.vector.tensor_tensor(out=sf[:, 0:4, 19:22], in0=c2[:], in1=sf[:, 0:4, 16:19], op=ALU.subtract)
-        nc.vector.tensor_copy(out=sf[:, 4:8, 0], in_=hq[:, 0, :])
-        nc.vector.tensor_copy(out=sf[:, 4:8, 16], in_=kn[:, 0, :])
-        nc.vector.tensor_tensor(out=sf[:, 4:8, 19], in0=kn[:, 0, :], in1=sf[:, 4:8, 16], op=ALU.subtract)
+        nc.vector.scalar_tensor_tensor(
+            out=kn[:], in0=vv[:, 1:4, 0:4], scalar=-0.5, in1=cv, op0=ALU.mult, op1=ALU.mult
+        )
+        turn_z(0, nc.vector.tensor_copy)
+        turn_z(1, nc.vector.tensor_copy)
+        st_ps = psum.tile([P, 8, P], BF16, tag="e")
+        for k in range(8):
+            nc.tensor.transpose(st_ps[:, k, :], sf[:, k, :], ident[:])
+        sT = keep.tile([P, 8, P], BF16, align_bytes=64)
+        nc.scalar.copy(out=sT[:], in_=st_ps[:])
 
         a_sb = keep.tile([P, 4096], U8, align_bytes=64)
         as_sb = keep.tile([P, 2048], U8, align_bytes=64)
@@ -151,12 +168,6 @@ def tile_hermitegaussianrbfimplicitshapespace_x2_kernel(
         zs = keep.tile([P, S], U8, align_bytes=64)
         nc.vector.quantize_mx(out=zc[:].bitcast(FP8X4), scales=zs[:], in_=zg[:].rearrange("p s t -> p (s t)"))
 
-
-        st_ps = psum.tile([P, 8, P], BF16, tag="e")
-        for k in range(8):
-            nc.tensor.transpose(st_ps[:, k, :], sf[:, k, :], ident[:])
-        sT = keep.tile([P, 8, P], BF16, align_bytes=64)
-        nc.scalar.copy(out=sT[:], in_=st_ps[:])
 
         psi = keep.tile([P, 4, N], F32, align_bytes=64)
 
@@ -176,12 +187,26 @@ def tile_hermitegaussianrbfimplicitshapespace_x2_kernel(
                     spread[c][:, P * nt : P * nt + P], xn[:, nt, c : c + 1].to_broadcast([P, P]), ident[:]
                 )
 
-        def make_slopes(c):
+        xb = keep.tile([P, 2, N], BF16, align_bytes=64)
+
+        def keep_points(c, cols):
+            nc.scalar.copy(out=xb[:, c - 1, cols], in_=spread[c][:, cols])
+
+        def make_slopes(c, cols):
             for j in range(4):
                 nc.scalar.activation(
-                    out=pc[:, c - 1, j, :], in_=spread[c][:], func=ACTF.Identity,
+                    out=pc[:, c - 1, j, cols], in_=spread[c][:, cols], func=ACTF.Identity,
                     bias=kn[:, c, j : j + 1], scale=hq[:, c, j : j + 1],
                 )
+
+        def pool_slopes(c, cols):
+            for j in range(4):
+                nc.gpsimd.tensor_scalar(
+                    out=pc[:, c - 1, j, cols], in0=xb[:, c - 1, cols],
+                    scalar1=hq[:, c, j : j + 1], scalar2=kn[:, c, j : j + 1], op0=ALU.mult, op1=ALU.add,
+                )
+
+        front, back = slice(0, 512), slice(512, N)
 
         wc = keep.tile([P, G, S], U32, align_bytes=64)
         ws = keep.tile([P, G, S], U8, align_bytes=64)
@@ -214,23 +239,43 @@ def tile_hermitegaussianrbfimplicitshapespace_x2_kernel(
                 out=wc[:, g, :].bitcast(FP8X4), scales=ws[:, g, :], in_=wb[:].rearrange("p s t -> p (s t)")
             )
 
+        w3 = keep.tile([P, 4, S], BF16, align_bytes=64)
+
+        def w_slots(g, h):
+            cols = slice(256 * h, 256 * h + 256)
+            for tt in range(2):
+                w_ps = psum.tile([P, 2, 256], F32, tag="p")
+                for t in range(2):
+                    w_matmul(w_ps[:, t, :], 4 * g + 2 * tt + t, cols)
+                for t in range(2):
+                    s = 2 * tt + t
+                    nc.scalar.activation(
+                        out=w3[:, s, cols], in_=w_ps[:, t, :], func=ACTF.Identity, bias=vv[:, 4 + g, s : s + 1], scale=1.0
+                    )
+
+        def w_join(h, wb):
+            cols = slice(256 * h, 256 * h + 256)
+            nc.scalar.copy(out=fours(wb[:, cols, :]), in_=slots(w3[:, :, cols]))
+
         wbs = [work.tile([P, S, 4], BF16, align_bytes=64, bufs=4, name="wb") for g in range(G)]
+        make_psi(0)
         extra = {
-            0: lambda: (order_a(1, nc.vector), make_psi(0)),
-            1: lambda: (spread_points(1), order_a(2, nc.vector), make_psi(1)),
-            2: lambda: (make_slopes(1), order_a(3, nc.vector)),
-            3: lambda: spread_points(2),
-            5: lambda: make_psi(2),
-            6: lambda: make_slopes(2),
-            7: lambda: make_psi(3),
+            0: lambda: (order_a(1, nc.vector), spread_points(2), keep_points(2, slice(0, N)),),
+            1: lambda: (make_psi(1), order_a(3, nc.vector), pool_slopes(2, front), pool_slopes(2, back),),
+            2: lambda: (spread_points(1), order_a(2, nc.vector),),
+            3: lambda: (make_slopes(1, slice(0, N)),),
+            4: lambda: (w_slots(3, 1),),
+            5: lambda: (make_psi(2),),
+            6: lambda: (w_join(1, wbs[3]),),
+            7: lambda: (make_psi(3),),
         }
-        for g in range(4):
-            for u in range(4):
-                w_quarter(g, u, wbs[g])
-                if g > 0 and u == 0:
-                    w_quant(g - 1, wbs[g - 1])
-                if 4 * g + u in extra:
-                    extra[4 * g + u]()
+        for k in range(14):
+            g, u = k // 4, k % 4
+            w_quarter(g, u, wbs[g])
+            if g > 0 and u == 0:
+                w_quant(g - 1, wbs[g - 1])
+            if k in extra:
+                extra[k]()
 
         kc = keep.tile([P, NT // 2, G, 2 * P], U32, align_bytes=64)
         ks = keep.tile([P, NT // 2, G, 2 * P], U8, align_bytes=64)
@@ -318,17 +363,17 @@ def tile_hermitegaussianrbfimplicitshapespace_x2_kernel(
         def join_out(h, copy, cols):
             copy(out=fours(o_bf[h][:, cols, :]), in_=slots(of[:, h, :, cols]))
 
-        def quant_out(h, cols):
+        def quant_out(h, cols, queue):
             nc.vector.quantize_mx(
                 out=ocs[h][:, cols].bitcast(FP8X4), scales=oss[h][:, cols], in_=o_bf[h][:, cols, :].rearrange("p m t -> p (m t)")
             )
-            nc.sync.dma_start(
+            queue.dma_start(
                 out=out_1[h][:, cols, :].rearrange("p m t -> p (m t)").bitcast(I32), in_=ocs[h][:, cols].bitcast(I32)
             )
 
-        def store_scales(h):
+        def store_scales(h, queues):
             for Q in range(4):
-                nc.sync.dma_start(
+                queues[Q % 2].dma_start(
                     out=out_2[h][4 * Q : 4 * Q + 4, :].bitcast(I32),
                     in_=oss[h][32 * Q : 32 * Q + 4, :].bitcast(I32),
                 )
@@ -358,6 +403,7 @@ def tile_hermitegaussianrbfimplicitshapespace_x2_kernel(
             if i > 0:
                 for nt in range(*groups[i - 1]):
                     stage2(nt)
+        join_out(0, nc.scalar.copy, slice(0, S))
         second_block(6, 7, kbs[3])
         slopes_0(7, 8)
         quant_pair(4, kbs[2])
@@ -371,8 +417,9 @@ def tile_hermitegaussianrbfimplicitshapespace_x2_kernel(
         quant_block(6, 2, kbs[3])
         second_block(7, 8, kbs[4])
         quant_block(6, 3, kbs[3])
-        join_out(0, nc.scalar.copy, slice(0, S))
         stage2(6)
+        quant_out(0, slice(0, S), nc.sync)
+        store_scales(0, (nc.sync, nc.sync))
         other_block(7, 8, 0, kbs[4])
         quant_block(7, 0, kbs[4])
         quant_block(7, 1, kbs[4])
@@ -383,8 +430,6 @@ def tile_hermitegaussianrbfimplicitshapespace_x2_kernel(
         for g in range(G):
             for h in range(2):
                 stage2_pass(ends[h][:], 7, g, slice(256 * h, 256 * h + 256), g == 0, g == G - 1)
-        quant_out(0, slice(0, S))
-        store_scales(0)
         for h, copy in ((0, nc.vector.tensor_copy), (1, nc.scalar.copy)):
             cols = slice(256 * h, 256 * h + 256)
             copy(out=of[:, 1, 3, cols], in_=ends[h][:])
@@ -392,6 +437,6 @@ def tile_hermitegaussianrbfimplicitshapespace_x2_kernel(
         join_out(1, nc.vector.tensor_copy, slice(0, 256))
         join_out(1, nc.scalar.copy, slice(384, S))
         join_out(1, nc.vector.tensor_copy, slice(256, 384))
-        quant_out(1, slice(0, 256))
-        quant_out(1, slice(256, S))
-        store_scales(1)
+        quant_out(1, slice(0, 256), nc.sync)
+        quant_out(1, slice(256, S), nc.scalar)
+        store_scales(1, (nc.sync, nc.scalar))

@@ -52,12 +52,12 @@ def tile_hermitegaussianrbfimplicitshapespace_x2_kernel(
         )
         z_rows = z.rearrange("(u p) d -> p u d", p=P)
         nc.sync.dma_start(out=z_sb[:, 0:2, :], in_=z_rows[:, 0:2, :])
-        nc.scalar.dma_start(out=vrow[0:4, 0:512], in_=q.rearrange("(g m) -> g m", g=4))
-        nc.scalar.dma_start(out=vrow[4:8, 0:512], in_=b.rearrange("(g m) -> g m", g=4))
         nc.scalar.dma_start(
             out=vrow[0:4, 512:896].rearrange("j (b x) -> j b x", x=24),
             in_=cen.rearrange("(b j i) c -> j b (i c)", j=4, i=8),
         )
+        nc.scalar.dma_start(out=vrow[0:4, 0:512], in_=q.rearrange("(g m) -> g m", g=4))
+        nc.scalar.dma_start(out=vrow[4:8, 0:512], in_=b.rearrange("(g m) -> g m", g=4))
         nc.sync.dma_start(out=z_sb[:, 2:4, :], in_=z_rows[:, 2:4, :])
         for h in range(2):
             cols = slice(2048 * h, 2048 * h + 2048)
@@ -71,49 +71,76 @@ def tile_hermitegaussianrbfimplicitshapespace_x2_kernel(
         make_identity(nc, ident[:])
         ident32 = keep.tile([P, P], F32, align_bytes=64)
         make_identity(nc, ident32[:])
-
         warm = keep.tile([P, 1], F32)
         nc.gpsimd.memset(warm[:], 0.0)
         nc.scalar.activation(out=warm[:], in_=warm[:], func=ACTF.Exp)
-        vzero = keep.tile([P, 512], BF16, align_bytes=64)
-        nc.vector.memset(vzero[:].bitcast(I32), 0)
-        sums = keep.tile([P, 2, 4, C], F32)
-        nc.vector.memset(sums[:], 0.0)
+
         xf = keep.tile([P, NT, P], BF16, align_bytes=64)
         nc.vector.memset(xf[:].bitcast(I32), 0)
         nc.vector.memset(xf[:, :, 16:22], 1.0)
         sf = keep.tile([P, 8, P], BF16, align_bytes=64)
         nc.vector.memset(sf[:].bitcast(I32), 0)
         nc.vector.memset(sf[:, 0:4, 32:38], -0.25)
-        chill = psum.tile([P, 512], F32, tag="o")
-        for k in range(3):
-            nc.tensor.matmul(chill[:], lhsT=vzero[:, 0:P], rhs=vzero[:], start=True, stop=True)
+        sums = keep.tile([P, 2, 4, C], F32)
+        nc.vector.memset(sums[:], 0.0)
         nc.scalar.copy(out=xf[:, :, 0:3], in_=xn[:])
         x2 = keep.tile([P, NT, C], F32)
         nc.vector.tensor_tensor(out=x2[:], in0=xn[:], in1=xn[:], op=ALU.mult)
         nc.vector.tensor_copy(out=xf[:, :, 32:35], in_=x2[:])
         nc.vector.tensor_tensor(out=xf[:, :, 35:38], in0=x2[:], in1=xf[:, :, 32:35], op=ALU.subtract)
-
         vord = keep.tile([P, 4, P], BF16, align_bytes=64)
         nc.vector.tensor_copy(
             out=vord[:].rearrange("p t (b i) -> p t b i", i=8),
             in_=vrow[:, 0:512].rearrange("p (b t i) -> p t b i", t=4, i=8),
         )
+        spread = {}
+
+        def spread_points(c):
+            spread[c] = psum.tile([P, N], BF16, tag="o", name="xb_ps")
+            for nt in range(NT):
+                nc.tensor.transpose(
+                    spread[c][:, P * nt : P * nt + P], xn[:, nt, c : c + 1].to_broadcast([P, P]), ident[:]
+                )
+
+        spread_points(1)
         v_ps = psum.tile([P, 7, P], BF16, tag="w")
         for c in range(C):
             nc.tensor.transpose(v_ps[:, 4 + c, :], vrow[:, 512 + c : 896 : 3], ident[:])
         for t in range(4):
             nc.tensor.transpose(v_ps[:, t, :], vord[:, t, :], ident[:])
-        xt_ps = psum.tile([P, NT, P], BF16, tag="e")
-        for nt in range(NT):
-            nc.tensor.transpose(xt_ps[:, nt, :], xf[:, nt, :], ident[:])
-        xt = keep.tile([P, NT, P], BF16, align_bytes=64)
-        nc.scalar.copy(out=xt[:], in_=xt_ps[:])
         vv = keep.tile([P, 8, 7], F32)
         nc.vector.tensor_copy(out=vv[:], in_=v_ps[:, :, 0:8].rearrange("p k r -> p r k"))
         cvj = vv[:, 0:4, 4:7]
         cv = cvj.rearrange("p j c -> p c j")
+        hq = keep.tile([P, C, 4], F32)
+        nc.scalar.mul(out=sf[:, 0:4, 0:3], in_=cvj, mul=0.5)
+        nc.scalar.mul(out=sf[:, 4:8, 0], in_=vv[:, 1, 0:4], mul=0.5)
+        nc.scalar.mul(out=hq[:], in_=vv[:, 1:4, 0:4], mul=0.5)
+        nc.vector.scalar_tensor_tensor(
+            out=sums[:, 0], in0=cvj, scalar=-0.25, in1=cvj, op0=ALU.mult, op1=ALU.mult
+        )
+        nc.vector.scalar_tensor_tensor(
+            out=sums[:, 1, :, 0], in0=vv[:, 1, 0:4], scalar=-0.5, in1=cv[:, 0, :], op0=ALU.mult, op1=ALU.mult
+        )
+        kn = keep.tile([P, C, 4], F32)
+        nc.vector.scalar_tensor_tensor(
+            out=kn[:], in0=vv[:, 1:4, 0:4], scalar=-0.5, in1=cv, op0=ALU.mult, op1=ALU.mult
+        )
+        high = sf[:, :, 16:19]
+        sums_rows = sums[:].rearrange("p e j c -> p (e j) c")
+        nc.vector.tensor_copy(out=high, in_=sums_rows)
+        nc.vector.tensor_tensor(out=sf[:, :, 19:22], in0=sums_rows, in1=high, op=ALU.subtract)
 
+        pc = keep.tile([P, 2, 4, N], F32, align_bytes=64)
+        def make_slopes(c, n0, n1):
+            cols = slice(P * n0, P * n1)
+            for j in range(4):
+                nc.scalar.activation(
+                    out=pc[:, c - 1, j, cols], in_=spread[c][:, cols], func=ACTF.Identity,
+                    bias=kn[:, c, j : j + 1], scale=hq[:, c, j : j + 1],
+                )
+
+        make_slopes(1, 0, 8)
         zw = z_sb[:].rearrange("p u d -> p (u d)").bitcast(F32)
         zg = keep.tile([P, S, 4], BF16, align_bytes=64)
         zgw = zg[:].rearrange("p s t -> p (s t)").bitcast(F32).rearrange("p (h v s u) -> p h v s u", h=2, v=2, u=2)
@@ -126,48 +153,34 @@ def tile_hermitegaussianrbfimplicitshapespace_x2_kernel(
                     nc.tensor.transpose(z_ps[:, v, u, :], zw[:, base + u : base + 256 : 2], ident32[:])
             copy(out=zgw[:, h], in_=z_ps[:].rearrange("p v u s -> p v s u"))
 
-        hq = keep.tile([P, C, 4], F32)
-        nc.vector.scalar_tensor_tensor(
-            out=sums[:, 0], in0=cvj, scalar=-0.25, in1=cvj, op0=ALU.mult, op1=ALU.mult
-        )
-        nc.vector.scalar_tensor_tensor(
-            out=sums[:, 1, :, 0], in0=vv[:, 1, 0:4], scalar=-0.5, in1=cv[:, 0, :], op0=ALU.mult, op1=ALU.mult
-        )
-        nc.scalar.mul(out=sf[:, 0:4, 0:3], in_=cvj, mul=0.5)
-        nc.scalar.mul(out=sf[:, 4:8, 0], in_=vv[:, 1, 0:4], mul=0.5)
-        high = sf[:, :, 16:19]
-        sums_rows = sums[:].rearrange("p e j c -> p (e j) c")
-        nc.vector.tensor_copy(out=high, in_=sums_rows)
-        nc.vector.tensor_tensor(out=sf[:, :, 19:22], in0=sums_rows, in1=high, op=ALU.subtract)
-        nc.scalar.mul(out=hq[:], in_=vv[:, 1:4, 0:4], mul=0.5)
-        kn = keep.tile([P, C, 4], F32)
-        nc.vector.scalar_tensor_tensor(
-            out=kn[:], in0=vv[:, 1:4, 0:4], scalar=-0.5, in1=cv, op0=ALU.mult, op1=ALU.mult
-        )
+        xt_ps = psum.tile([P, NT, P], BF16, tag="e")
+        xt = keep.tile([P, NT, P], BF16, align_bytes=64)
         turn_z(0, nc.vector.tensor_copy)
+        for nt in range(NT):
+            nc.tensor.transpose(xt_ps[:, nt, :], xf[:, nt, :], ident[:])
+        nc.vector.tensor_copy(out=xt[:], in_=xt_ps[:])
         turn_z(1, nc.vector.tensor_copy)
         st_ps = psum.tile([P, 8, P], BF16, tag="e")
         for k in range(8):
             nc.tensor.transpose(st_ps[:, k, :], sf[:, k, :], ident[:])
         sT = keep.tile([P, 8, P], BF16, align_bytes=64)
-        nc.scalar.copy(out=sT[:], in_=st_ps[:])
 
         a_sb = keep.tile([P, 4096], U8, align_bytes=64)
         as_sb = keep.tile([P, 2048], U8, align_bytes=64)
 
-        def order_a(g, eng):
+        def order_a(g):
             for dst, raw, w in ((a_sb, a_raw, 4), (as_sb, as_raw, 2)):
                 n = 64 * w
-                eng.tensor_copy(
+                nc.vector.tensor_copy(
                     out=dst[:].bitcast(I32)[:, g * n : g * n + n].rearrange("p (t b w) -> p t b w", t=4, w=w),
                     in_=raw[:].bitcast(I32)[:, g * n : g * n + n].rearrange("p (b t w) -> p t b w", t=4, w=w),
                 )
 
-        order_a(0, nc.vector)
+        order_a(0)
         zc = keep.tile([P, S], U32, align_bytes=64)
         zs = keep.tile([P, S], U8, align_bytes=64)
         nc.vector.quantize_mx(out=zc[:].bitcast(FP8X4), scales=zs[:], in_=zg[:].rearrange("p s t -> p (s t)"))
-
+        nc.vector.tensor_copy(out=sT[:], in_=st_ps[:])
 
         psi = keep.tile([P, 4, N], F32, align_bytes=64)
 
@@ -177,39 +190,9 @@ def tile_hermitegaussianrbfimplicitshapespace_x2_kernel(
                 nc.tensor.matmul(e_ps[:, j, :], lhsT=sT[:, j, :], rhs=xt[:, nt, :], start=True, stop=True)
             nc.scalar.activation(out=psi[:, :, P * nt : P * nt + P], in_=e_ps[:], func=ACTF.Exp)
 
-        pc = keep.tile([P, 2, 4, N], F32, align_bytes=64)
-        spread = {}
-
-        def spread_points(c):
-            spread[c] = psum.tile([P, N], BF16, tag="o", name="xb_ps")
-            for nt in range(NT):
-                nc.tensor.transpose(
-                    spread[c][:, P * nt : P * nt + P], xn[:, nt, c : c + 1].to_broadcast([P, P]), ident[:]
-                )
-
-        xb = keep.tile([P, 2, N], BF16, align_bytes=64)
-
-        def keep_points(c, cols):
-            nc.scalar.copy(out=xb[:, c - 1, cols], in_=spread[c][:, cols])
-
-        def make_slopes(c, cols):
-            for j in range(4):
-                nc.scalar.activation(
-                    out=pc[:, c - 1, j, cols], in_=spread[c][:, cols], func=ACTF.Identity,
-                    bias=kn[:, c, j : j + 1], scale=hq[:, c, j : j + 1],
-                )
-
-        def pool_slopes(c, cols):
-            for j in range(4):
-                nc.gpsimd.tensor_scalar(
-                    out=pc[:, c - 1, j, cols], in0=xb[:, c - 1, cols],
-                    scalar1=hq[:, c, j : j + 1], scalar2=kn[:, c, j : j + 1], op0=ALU.mult, op1=ALU.add,
-                )
-
-        front, back = slice(0, 512), slice(512, N)
-
         wc = keep.tile([P, G, S], U32, align_bytes=64)
         ws = keep.tile([P, G, S], U8, align_bytes=64)
+        wbs = [work.tile([P, S, 4], BF16, align_bytes=64, bufs=4, name="wb") for g in range(G)]
 
         def w_matmul(out, k, cols):
             nc.tensor.matmul_mx(
@@ -222,21 +205,21 @@ def tile_hermitegaussianrbfimplicitshapespace_x2_kernel(
                 stop=True,
             )
 
-        def w_quarter(g, u, wb):
+        def w_quarter(g, u):
             w_ps = psum.tile([P, 4, P], F32, tag="w")
             cols = slice(P * u, P * u + P)
             for t in range(4):
                 w_matmul(w_ps[:, t, :], 4 * g + t, cols)
             nc.vector.tensor_tensor(
-                out=wb[:, cols, :],
+                out=wbs[g][:, cols, :],
                 in0=w_ps[:].rearrange("p t s -> p s t"),
                 in1=vv[:, 4 + g : 5 + g, 0:4].to_broadcast([P, P, 4]),
                 op=ALU.add,
             )
 
-        def w_quant(g, wb):
+        def w_quant(g):
             nc.vector.quantize_mx(
-                out=wc[:, g, :].bitcast(FP8X4), scales=ws[:, g, :], in_=wb[:].rearrange("p s t -> p (s t)")
+                out=wc[:, g, :].bitcast(FP8X4), scales=ws[:, g, :], in_=wbs[g][:].rearrange("p s t -> p (s t)")
             )
 
         w3 = keep.tile([P, 4, S], BF16, align_bytes=64)
@@ -253,27 +236,25 @@ def tile_hermitegaussianrbfimplicitshapespace_x2_kernel(
                         out=w3[:, s, cols], in_=w_ps[:, t, :], func=ACTF.Identity, bias=vv[:, 4 + g, s : s + 1], scale=1.0
                     )
 
-        def w_join(h, wb):
+        def w_join(g, h):
             cols = slice(256 * h, 256 * h + 256)
-            nc.scalar.copy(out=fours(wb[:, cols, :]), in_=slots(w3[:, :, cols]))
+            nc.scalar.copy(out=fours(wbs[g][:, cols, :]), in_=slots(w3[:, :, cols]))
 
-        wbs = [work.tile([P, S, 4], BF16, align_bytes=64, bufs=4, name="wb") for g in range(G)]
-        make_psi(0)
+
         extra = {
-            0: lambda: (order_a(1, nc.vector), spread_points(2), keep_points(2, slice(0, N)),),
-            1: lambda: (make_psi(1), order_a(3, nc.vector), pool_slopes(2, front), pool_slopes(2, back),),
-            2: lambda: (spread_points(1), order_a(2, nc.vector),),
-            3: lambda: (make_slopes(1, slice(0, N)),),
-            4: lambda: (w_slots(3, 1),),
-            5: lambda: (make_psi(2),),
-            6: lambda: (w_join(1, wbs[3]),),
-            7: lambda: (make_psi(3),),
+            0: lambda: (make_psi(0), order_a(3),),
+            1: lambda: (make_psi(1), order_a(1),),
+            2: lambda: (w_slots(3, 0), spread_points(2),),
+            3: lambda: (w_join(3, 0), order_a(2),),
+            4: lambda: (w_slots(3, 1), w_join(3, 1),),
+            6: lambda: (make_slopes(2, 0, 4), make_psi(2),),
+            8: lambda: (make_psi(3),),
         }
-        for k in range(14):
+        for k in range(12):
             g, u = k // 4, k % 4
-            w_quarter(g, u, wbs[g])
+            w_quarter(g, u)
             if g > 0 and u == 0:
-                w_quant(g - 1, wbs[g - 1])
+                w_quant(g - 1)
             if k in extra:
                 extra[k]()
 
@@ -382,8 +363,19 @@ def tile_hermitegaussianrbfimplicitshapespace_x2_kernel(
         later_psi = {0: [4, 5], 1: [6, 7]}
         kbs = [work.tile([P, G, 2 * P, 4], BF16, align_bytes=64, bufs=5, name="kb") for i in groups]
 
+        on_vector = (4,)
+
         def first(i):
-            first_block(*groups[i], scaled_psi(*groups[i]), kbs[i])
+            n0, n1 = groups[i]
+            if i in on_vector:
+                nc.vector.tensor_tensor(
+                    out=fours(kbs[i][:, 0, 0 : P * (n1 - n0), :]),
+                    in0=slots(psi[:, :, P * n0 : P * n1]),
+                    in1=vv[:, 0:1, 0:4].unsqueeze(3).to_broadcast([P, 32 * (n1 - n0), 4, 4]),
+                    op=ALU.mult,
+                )
+            else:
+                first_block(n0, n1, scaled_psi(n0, n1), kbs[i])
 
         first(0)
         slopes_0(0, 2)
@@ -392,9 +384,12 @@ def tile_hermitegaussianrbfimplicitshapespace_x2_kernel(
             second_block(n0, n1, kbs[i])
             slopes_0(*groups[i + 1])
             if i == 0:
-                w_quant(3, wbs[3])
+                w_quant(2)
+                w_quant(3)
             else:
                 quant_pair(groups[i - 1][0], kbs[i - 1])
+            if i == 0:
+                make_slopes(2, 4, 8)
             for nt in later_psi.get(i, ()):
                 make_psi(nt)
             first(i + 1)
@@ -435,8 +430,8 @@ def tile_hermitegaussianrbfimplicitshapespace_x2_kernel(
             copy(out=of[:, 1, 3, cols], in_=ends[h][:])
             nc.sync.dma_start(out=out_rows[1, 3][:, cols], in_=of[:, 1, 3, cols])
         join_out(1, nc.vector.tensor_copy, slice(0, 256))
-        join_out(1, nc.scalar.copy, slice(384, S))
-        join_out(1, nc.vector.tensor_copy, slice(256, 384))
+        join_out(1, nc.scalar.copy, slice(320, S))
+        join_out(1, nc.vector.tensor_copy, slice(256, 320))
         quant_out(1, slice(0, 256), nc.sync)
-        quant_out(1, slice(256, S), nc.scalar)
-        store_scales(1, (nc.sync, nc.scalar))
+        quant_out(1, slice(256, S), nc.sync)
+        store_scales(1, (nc.sync, nc.sync))

@@ -40,14 +40,19 @@ def tile_hermitegaussianrbfimplicitshapespace_x2_kernel(
         ctx.enter_context(tc.manual_schedule())
 
         vrow = keep.tile([P, 896], BF16, align_bytes=64)
-        xn = keep.tile([P, NT, C], BF16, align_bytes=64)
+        xn = keep.tile([P, 2, 16], BF16, align_bytes=64)
         z_sb = keep.tile([P, 4, D], BF16, align_bytes=64)
         a_raw = keep.tile([P, 4096], U8, align_bytes=64)
         as_raw = keep.tile([P, 2048], U8, align_bytes=64)
+        idle = keep.tile([P, P], F32, align_bytes=64)
+        nc.vector.memset(idle[:], 0.0)
         nc.vector.memset(vrow[:].bitcast(I32), 0)
+        spin = psum.tile([P, P], F32, tag="p")
+        for k in range(4):
+            nc.tensor.matmul(spin[:], lhsT=idle[:], rhs=idle[:], start=True, stop=True)
         nc.gpsimd.memset(as_raw[:].bitcast(I32), 0)
         nc.scalar.dma_start(
-            out=xn[:].rearrange("p (g t) c -> p g (t c)", g=2),
+            out=xn[:, :, 0:12],
             in_=x.rearrange("(g p t) c -> p g (t c)", g=2, t=4),
         )
         z_rows = z.rearrange("(u p) d -> p u d", p=P)
@@ -83,11 +88,13 @@ def tile_hermitegaussianrbfimplicitshapespace_x2_kernel(
         nc.vector.memset(sf[:, 0:4, 32:38], -0.25)
         sums = keep.tile([P, 2, 4, C], F32)
         nc.vector.memset(sums[:], 0.0)
-        nc.scalar.copy(out=xf[:, :, 0:3], in_=xn[:])
-        x2 = keep.tile([P, NT, C], F32)
-        nc.vector.tensor_tensor(out=x2[:], in0=xn[:], in1=xn[:], op=ALU.mult)
-        nc.vector.tensor_copy(out=xf[:, :, 32:35], in_=x2[:])
-        nc.vector.tensor_tensor(out=xf[:, :, 35:38], in0=x2[:], in1=xf[:, :, 32:35], op=ALU.subtract)
+        points = xn[:, :, 0:12].rearrange("p g (t c) -> p g t c", c=C)
+        nc.scalar.copy(out=xf[:, :, 0:3].rearrange("p (g t) c -> p g t c", g=2), in_=points)
+        x2 = keep.tile([P, 2, 12], F32)
+        nc.vector.tensor_tensor(out=x2[:], in0=xn[:, :, 0:12], in1=xn[:, :, 0:12], op=ALU.mult)
+        squares = x2[:].rearrange("p g (t c) -> p (g t) c", c=C)
+        nc.vector.tensor_copy(out=xf[:, :, 32:35], in_=squares)
+        nc.vector.tensor_tensor(out=xf[:, :, 35:38], in0=squares, in1=xf[:, :, 32:35], op=ALU.subtract)
         vord = keep.tile([P, 4, P], BF16, align_bytes=64)
         nc.vector.tensor_copy(
             out=vord[:].rearrange("p t (b i) -> p t b i", i=8),
@@ -99,7 +106,7 @@ def tile_hermitegaussianrbfimplicitshapespace_x2_kernel(
             spread[c] = psum.tile([P, N], BF16, tag="o", name="xb_ps")
             for nt in range(NT):
                 nc.tensor.transpose(
-                    spread[c][:, P * nt : P * nt + P], xn[:, nt, c : c + 1].to_broadcast([P, P]), ident[:]
+                    spread[c][:, P * nt : P * nt + P], xn[:, nt // 4, C * (nt % 4) + c : C * (nt % 4) + c + 1].to_broadcast([P, P]), ident[:]
                 )
 
         spread_points(1)
@@ -156,10 +163,9 @@ def tile_hermitegaussianrbfimplicitshapespace_x2_kernel(
         xt_ps = psum.tile([P, NT, P], BF16, tag="e")
         xt = keep.tile([P, NT, P], BF16, align_bytes=64)
         turn_z(0, nc.vector.tensor_copy)
+        turn_z(1, nc.vector.tensor_copy)
         for nt in range(NT):
             nc.tensor.transpose(xt_ps[:, nt, :], xf[:, nt, :], ident[:])
-        nc.vector.tensor_copy(out=xt[:], in_=xt_ps[:])
-        turn_z(1, nc.vector.tensor_copy)
         st_ps = psum.tile([P, 8, P], BF16, tag="e")
         for k in range(8):
             nc.tensor.transpose(st_ps[:, k, :], sf[:, k, :], ident[:])
@@ -180,6 +186,7 @@ def tile_hermitegaussianrbfimplicitshapespace_x2_kernel(
         zc = keep.tile([P, S], U32, align_bytes=64)
         zs = keep.tile([P, S], U8, align_bytes=64)
         nc.vector.quantize_mx(out=zc[:].bitcast(FP8X4), scales=zs[:], in_=zg[:].rearrange("p s t -> p (s t)"))
+        nc.vector.tensor_copy(out=xt[:], in_=xt_ps[:])
         nc.vector.tensor_copy(out=sT[:], in_=st_ps[:])
 
         psi = keep.tile([P, 4, N], F32, align_bytes=64)
@@ -242,11 +249,11 @@ def tile_hermitegaussianrbfimplicitshapespace_x2_kernel(
 
 
         extra = {
-            0: lambda: (make_psi(0), order_a(3),),
-            1: lambda: (make_psi(1), order_a(1),),
-            2: lambda: (w_slots(3, 0), spread_points(2),),
+            0: lambda: (order_a(3),),
+            1: lambda: (make_psi(0), order_a(1),),
+            2: lambda: (w_slots(3, 0), make_psi(1),),
             3: lambda: (w_join(3, 0), order_a(2),),
-            4: lambda: (w_slots(3, 1), w_join(3, 1),),
+            4: lambda: (w_slots(3, 1), w_join(3, 1), spread_points(2),),
             6: lambda: (make_slopes(2, 0, 4), make_psi(2),),
             8: lambda: (make_psi(3),),
         }

from contextlib import ExitStack

import concourse.mybir as mybir
from concourse.masks import make_identity

F32 = mybir.dt.float32
BF16 = mybir.dt.bfloat16
I32 = mybir.dt.int32
U32 = mybir.dt.uint32
U8 = mybir.dt.uint8
FP8X4 = mybir.dt.float8_e4m3fn_x4
FP4X4 = mybir.dt.float4_e2m1fn_x4
ACTF = mybir.ActivationFunctionType
ALU = mybir.AluOpType

P = 128
N, M, S, D, C = 1024, 512, 512, 512, 3
G = C + 1
NT = N // P
FLOPS = 2 * S * D * G * M + 2 * N * S * G * M


def fours(ap):
    return ap.rearrange("p (a i) t -> p a t i", i=4)


def slots(ap):
    return ap.rearrange("p t (a i) -> p a t i", i=4)


def tile_hermitegaussianrbfimplicitshapespace_x2_kernel(
    tc, x, cen, z, a_words, a_scales, b, q, out_0, out_1, out_2
):
    nc = tc.nc
    with ExitStack() as ctx:
        keep = ctx.enter_context(tc.tile_pool(name="keep", bufs=1))
        work = ctx.enter_context(tc.tile_pool(name="work", bufs=3))
        psum = ctx.enter_context(tc.psum_pool(name="psum", bufs=2))

        ctx.enter_context(tc.manual_schedule())

        vrow = keep.tile([P, 896], BF16, align_bytes=64)
        xn = keep.tile([P, 2, 16], BF16, align_bytes=64)
        z_sb = keep.tile([P, 4, D], BF16, align_bytes=64)
        a_raw = keep.tile([P, 4096], U8, align_bytes=64)
        as_raw = keep.tile([P, 2048], U8, align_bytes=64)
        idle = keep.tile([P, P], F32, align_bytes=64)
        nc.vector.memset(idle[:], 0.0)
        nc.vector.memset(vrow[:].bitcast(I32), 0)
        spin = psum.tile([P, P], F32, tag="p")
        for k in range(4):
            nc.tensor.matmul(spin[:], lhsT=idle[:], rhs=idle[:], start=True, stop=True)
        nc.gpsimd.memset(as_raw[:].bitcast(I32), 0)
        nc.scalar.dma_start(
            out=xn[:, :, 0:12],
            in_=x.rearrange("(g p t) c -> p g (t c)", g=2, t=4),
        )
        z_rows = z.rearrange("(u p) d -> p u d", p=P)
        nc.sync.dma_start(out=z_sb[:, 0:2, :], in_=z_rows[:, 0:2, :])
        nc.scalar.dma_start(
            out=vrow[0:4, 512:896].rearrange("j (b x) -> j b x", x=24),
            in_=cen.rearrange("(b j i) c -> j b (i c)", j=4, i=8),
        )
        nc.scalar.dma_start(out=vrow[0:4, 0:512], in_=q.rearrange("(g m) -> g m", g=4))
        nc.scalar.dma_start(out=vrow[4:8, 0:512], in_=b.rearrange("(g m) -> g m", g=4))
        nc.sync.dma_start(out=z_sb[:, 2:4, :], in_=z_rows[:, 2:4, :])
        for h in range(2):
            cols = slice(2048 * h, 2048 * h + 2048)
            nc.sync.dma_start(out=a_raw[:, cols].bitcast(I32), in_=a_words[0][:, cols].bitcast(I32))
        for Q in range(4):
            nc.scalar.dma_start(
                out=as_raw[32 * Q : 32 * Q + 4, :].bitcast(I32),
                in_=a_scales[0][4 * Q : 4 * Q + 4, :].bitcast(I32),
            )
        ident = keep.tile([P, P], BF16, align_bytes=64)
        make_identity(nc, ident[:])
        ident32 = keep.tile([P, P], F32, align_bytes=64)
        make_identity(nc, ident32[:])
        warm = keep.tile([P, 1], F32)
        nc.gpsimd.memset(warm[:], 0.0)
        nc.scalar.activation(out=warm[:], in_=warm[:], func=ACTF.Exp)

        xf = keep.tile([P, NT, P], BF16, align_bytes=64)
        nc.vector.memset(xf[:].bitcast(I32), 0)
        nc.vector.memset(xf[:, :, 16:22], 1.0)
        sf = keep.tile([P, 8, P], BF16, align_bytes=64)
        nc.vector.memset(sf[:].bitcast(I32), 0)
        nc.vector.memset(sf[:, 0:4, 32:38], -0.25)
        sums = keep.tile([P, 2, 4, C], F32)
        nc.vector.memset(sums[:], 0.0)
        points = xn[:, :, 0:12].rearrange("p g (t c) -> p g t c", c=C)
        nc.scalar.copy(out=xf[:, :, 0:3].rearrange("p (g t) c -> p g t c", g=2), in_=points)
        x2 = keep.tile([P, 2, 12], F32)
        nc.vector.tensor_tensor(out=x2[:], in0=xn[:, :, 0:12], in1=xn[:, :, 0:12], op=ALU.mult)
        squares = x2[:].rearrange("p g (t c) -> p (g t) c", c=C)
        nc.vector.tensor_copy(out=xf[:, :, 32:35], in_=squares)
        nc.vector.tensor_tensor(out=xf[:, :, 35:38], in0=squares, in1=xf[:, :, 32:35], op=ALU.subtract)
        vord = keep.tile([P, 4, P], BF16, align_bytes=64)
        nc.vector.tensor_copy(
            out=vord[:].rearrange("p t (b i) -> p t b i", i=8),
            in_=vrow[:, 0:512].rearrange("p (b t i) -> p t b i", t=4, i=8),
        )
        spread = {}

        def spread_points(c):
            spread[c] = psum.tile([P, N], BF16, tag="o", name="xb_ps")
            for nt in range(NT):
                nc.tensor.transpose(
                    spread[c][:, P * nt : P * nt + P], xn[:, nt // 4, C * (nt % 4) + c : C * (nt % 4) + c + 1].to_broadcast([P, P]), ident[:]
                )

        spread_points(1)
        v_ps = psum.tile([P, 7, P], BF16, tag="w")
        for c in range(C):
            nc.tensor.transpose(v_ps[:, 4 + c, :], vrow[:, 512 + c : 896 : 3], ident[:])
        for t in range(4):
            nc.tensor.transpose(v_ps[:, t, :], vord[:, t, :], ident[:])
        vv = keep.tile([P, 8, 7], F32)
        nc.vector.tensor_copy(out=vv[:], in_=v_ps[:, :, 0:8].rearrange("p k r -> p r k"))
        cvj = vv[:, 0:4, 4:7]
        cv = cvj.rearrange("p j c -> p c j")
        hq = keep.tile([P, C, 4], F32)
        nc.scalar.mul(out=sf[:, 0:4, 0:3], in_=cvj, mul=0.5)
        nc.scalar.mul(out=sf[:, 4:8, 0], in_=vv[:, 1, 0:4], mul=0.5)
        nc.scalar.mul(out=hq[:], in_=vv[:, 1:4, 0:4], mul=0.5)
        nc.vector.scalar_tensor_tensor(
            out=sums[:, 0], in0=cvj, scalar=-0.25, in1=cvj, op0=ALU.mult, op1=ALU.mult
        )
        nc.vector.scalar_tensor_tensor(
            out=sums[:, 1, :, 0], in0=vv[:, 1, 0:4], scalar=-0.5, in1=cv[:, 0, :], op0=ALU.mult, op1=ALU.mult
        )
        kn = keep.tile([P, C, 4], F32)
        nc.vector.scalar_tensor_tensor(
            out=kn[:], in0=vv[:, 1:4, 0:4], scalar=-0.5, in1=cv, op0=ALU.mult, op1=ALU.mult
        )
        high = sf[:, :, 16:19]
        sums_rows = sums[:].rearrange("p e j c -> p (e j) c")
        nc.vector.tensor_copy(out=high, in_=sums_rows)
        nc.vector.tensor_tensor(out=sf[:, :, 19:22], in0=sums_rows, in1=high, op=ALU.subtract)

        pc = keep.tile([P, 2, 4, N], F32, align_bytes=64)
        def make_slopes(c, n0, n1):
            cols = slice(P * n0, P * n1)
            for j in range(4):
                nc.scalar.activation(
                    out=pc[:, c - 1, j, cols], in_=spread[c][:, cols], func=ACTF.Identity,
                    bias=kn[:, c, j : j + 1], scale=hq[:, c, j : j + 1],
                )

        make_slopes(1, 0, 8)
        zw = z_sb[:].rearrange("p u d -> p (u d)").bitcast(F32)
        zg = keep.tile([P, S, 4], BF16, align_bytes=64)
        zgw = zg[:].rearrange("p s t -> p (s t)").bitcast(F32).rearrange("p (h v s u) -> p h v s u", h=2, v=2, u=2)

        def turn_z(h, copy):
            z_ps = psum.tile([P, 2, 2, P], F32, tag="p")
            for v in range(2):
                base = 256 * (2 * h + v)
                for u in range(2):
                    nc.tensor.transpose(z_ps[:, v, u, :], zw[:, base + u : base + 256 : 2], ident32[:])
            copy(out=zgw[:, h], in_=z_ps[:].rearrange("p v u s -> p v s u"))

        xt_ps = psum.tile([P, NT, P], BF16, tag="e")
        xt = keep.tile([P, NT, P], BF16, align_bytes=64)
        turn_z(0, nc.vector.tensor_copy)
        turn_z(1, nc.vector.tensor_copy)
        for nt in range(NT):
            nc.tensor.transpose(xt_ps[:, nt, :], xf[:, nt, :], ident[:])
        st_ps = psum.tile([P, 8, P], BF16, tag="e")
        for k in range(8):
            nc.tensor.transpose(st_ps[:, k, :], sf[:, k, :], ident[:])
        sT = keep.tile([P, 8, P], BF16, align_bytes=64)

        a_sb = keep.tile([P, 4096], U8, align_bytes=64)
        as_sb = keep.tile([P, 2048], U8, align_bytes=64)

        def order_a(g):
            for dst, raw, w in ((a_sb, a_raw, 4), (as_sb, as_raw, 2)):
                n = 64 * w
                nc.vector.tensor_copy(
                    out=dst[:].bitcast(I32)[:, g * n : g * n + n].rearrange("p (t b w) -> p t b w", t=4, w=w),
                    in_=raw[:].bitcast(I32)[:, g * n : g * n + n].rearrange("p (b t w) -> p t b w", t=4, w=w),
                )

        order_a(0)
        zc = keep.tile([P, S], U32, align_bytes=64)
        zs = keep.tile([P, S], U8, align_bytes=64)
        nc.vector.quantize_mx(out=zc[:].bitcast(FP8X4), scales=zs[:], in_=zg[:].rearrange("p s t -> p (s t)"))
        nc.vector.tensor_copy(out=xt[:], in_=xt_ps[:])
        nc.vector.tensor_copy(out=sT[:], in_=st_ps[:])

        psi = keep.tile([P, 4, N], F32, align_bytes=64)

        def make_psi(nt):
            e_ps = psum.tile([P, 4, P], F32, tag="e")
            for j in range(4):
                nc.tensor.matmul(e_ps[:, j, :], lhsT=sT[:, j, :], rhs=xt[:, nt, :], start=True, stop=True)
            nc.scalar.activation(out=psi[:, :, P * nt : P * nt + P], in_=e_ps[:], func=ACTF.Exp)

        wc = keep.tile([P, G, S], U32, align_bytes=64)
        ws = keep.tile([P, G, S], U8, align_bytes=64)
        wbs = [work.tile([P, S, 4], BF16, align_bytes=64, bufs=4, name="wb") for g in range(G)]

        def w_matmul(out, k, cols):
            nc.tensor.matmul_mx(
                out=out,
                lhsT=a_sb[:, 256 * k : 256 * k + 256].bitcast(FP4X4),
                lhsT_scale=as_sb[:, P * k : P * k + P],
                rhs=zc[:, cols].bitcast(FP8X4),
                rhs_scale=zs[:, cols],
                start=True,
                stop=True,
            )

        def w_quarter(g, u):
            w_ps = psum.tile([P, 4, P], F32, tag="w")
            cols = slice(P * u, P * u + P)
            for t in range(4):
                w_matmul(w_ps[:, t, :], 4 * g + t, cols)
            nc.vector.tensor_tensor(
                out=wbs[g][:, cols, :],
                in0=w_ps[:].rearrange("p t s -> p s t"),
                in1=vv[:, 4 + g : 5 + g, 0:4].to_broadcast([P, P, 4]),
                op=ALU.add,
            )

        def w_quant(g):
            nc.vector.quantize_mx(
                out=wc[:, g, :].bitcast(FP8X4), scales=ws[:, g, :], in_=wbs[g][:].rearrange("p s t -> p (s t)")
            )

        w3 = keep.tile([P, 4, S], BF16, align_bytes=64)

        def w_slots(g, h):
            cols = slice(256 * h, 256 * h + 256)
            for tt in range(2):
                w_ps = psum.tile([P, 2, 256], F32, tag="p")
                for t in range(2):
                    w_matmul(w_ps[:, t, :], 4 * g + 2 * tt + t, cols)
                for t in range(2):
                    s = 2 * tt + t
                    nc.scalar.activation(
                        out=w3[:, s, cols], in_=w_ps[:, t, :], func=ACTF.Identity, bias=vv[:, 4 + g, s : s + 1], scale=1.0
                    )

        def w_join(g, h):
            cols = slice(256 * h, 256 * h + 256)
            nc.scalar.copy(out=fours(wbs[g][:, cols, :]), in_=slots(w3[:, :, cols]))


        extra = {
            0: lambda: (order_a(3),),
            1: lambda: (make_psi(0), order_a(1),),
            2: lambda: (w_slots(3, 0), make_psi(1),),
            3: lambda: (w_join(3, 0), order_a(2),),
            4: lambda: (w_slots(3, 1), w_join(3, 1), spread_points(2),),
            6: lambda: (make_slopes(2, 0, 4), make_psi(2),),
            8: lambda: (make_psi(3),),
        }
        for k in range(12):
            g, u = k // 4, k % 4
            w_quarter(g, u)
            if g > 0 and u == 0:
                w_quant(g - 1)
            if k in extra:
                extra[k]()

        kc = keep.tile([P, NT // 2, G, 2 * P], U32, align_bytes=64)
        ks = keep.tile([P, NT // 2, G, 2 * P], U8, align_bytes=64)
        of = keep.tile([P, 2, 4, S], F32, align_bytes=64)
        out_rows = out_0.rearrange("(g p t) m -> g t p m", g=2, t=4)

        def scaled_psi(n0, n1):
            kq0 = work.tile([P, 4, 2 * P], BF16, align_bytes=64, bufs=3)
            for j in range(4):
                nc.scalar.activation(
                    out=kq0[:, j, 0 : P * (n1 - n0)],
                    in_=psi[:, j, P * n0 : P * n1],
                    func=ACTF.Copy,
                    scale=vv[:, 0, j : j + 1],
                )
            return kq0

        def first_block(n0, n1, kq0, kb):
            nc.scalar.copy(out=fours(kb[:, 0, 0 : P * (n1 - n0), :]), in_=slots(kq0[:, :, 0 : P * (n1 - n0)]))

        slope = {}

        def slopes_0(n0, n1):
            for nt in range(n0, n1):
                p_ps = psum.tile([P, 4, P], F32, tag="p")
                slope[nt] = p_ps
                for j in range(4):
                    nc.tensor.matmul(p_ps[:, j, :], lhsT=sT[:, 4 + j, :], rhs=xt[:, nt, :], start=True, stop=True)

        def second_block(n0, n1, kb):
            for nt in range(n0, n1):
                nc.vector.tensor_tensor(
                    out=fours(kb[:, 1, P * (nt - n0) : P * (nt - n0) + P, :]),
                    in0=slots(slope[nt][:]),
                    in1=slots(psi[:, :, P * nt : P * nt + P]),
                    op=ALU.mult,
                )

        def other_block(n0, n1, c, kb):
            nc.vector.tensor_tensor(
                out=fours(kb[:, 2 + c, 0 : (n1 - n0) * P, :]),
                in0=slots(pc[:, c, :, P * n0 : P * n1]),
                in1=slots(psi[:, :, P * n0 : P * n1]),
                op=ALU.mult,
            )

        def quant_pair(n0, kb):
            nc.vector.quantize_mx(
                out=kc[:, n0 // 2].rearrange("p g n -> p (g n)").bitcast(FP8X4),
                scales=ks[:, n0 // 2].rearrange("p g n -> p (g n)"),
                in_=kb[:].rearrange("p g n t -> p (g n t)"),
            )

        def quant_block(nt, g, kb):
            off = P * (nt % 2)
            nc.vector.quantize_mx(
                out=kc[:, nt // 2, g, off : off + P].bitcast(FP8X4),
                scales=ks[:, nt // 2, g, off : off + P],
                in_=kb[:, g, 0:P, :].rearrange("p n t -> p (n t)"),
            )

        def stage2_pass(o_ap, nt, g, cols, first, last):
            off = P * (nt % 2)
            nc.tensor.matmul_mx(
                out=o_ap,
                lhsT=kc[:, nt // 2, g, off : off + P].bitcast(FP8X4),
                lhsT_scale=ks[:, nt // 2, g, off : off + P],
                rhs=wc[:, g, cols].bitcast(FP8X4),
                rhs_scale=ws[:, g, cols],
                start=first,
                stop=last,
            )

        def stage2(nt):
            o_ps = psum.tile([P, S], F32, tag="o")
            for g in range(G):
                stage2_pass(o_ps[:], nt, g, slice(0, S), g == 0, g == G - 1)
            nc.scalar.copy(out=of[:, nt // 4, nt % 4, :], in_=o_ps[:])
            nc.sync.dma_start(out=out_rows[nt // 4, nt % 4], in_=of[:, nt // 4, nt % 4, :])

        o_bf = [keep.tile([P, S, 4], BF16, align_bytes=64, name="ob%d" % h) for h in range(2)]
        ocs = [keep.tile([P, S], U32, align_bytes=64, name="oc%d" % h) for h in range(2)]
        oss = [keep.tile([P, S], U8, align_bytes=64, name="osc%d" % h) for h in range(2)]

        def join_out(h, copy, cols):
            copy(out=fours(o_bf[h][:, cols, :]), in_=slots(of[:, h, :, cols]))

        def quant_out(h, cols, queue):
            nc.vector.quantize_mx(
                out=ocs[h][:, cols].bitcast(FP8X4), scales=oss[h][:, cols], in_=o_bf[h][:, cols, :].rearrange("p m t -> p (m t)")
            )
            queue.dma_start(
                out=out_1[h][:, cols, :].rearrange("p m t -> p (m t)").bitcast(I32), in_=ocs[h][:, cols].bitcast(I32)
            )

        def store_scales(h, queues):
            for Q in range(4):
                queues[Q % 2].dma_start(
                    out=out_2[h][4 * Q : 4 * Q + 4, :].bitcast(I32),
                    in_=oss[h][32 * Q : 32 * Q + 4, :].bitcast(I32),
                )

        groups = [(0, 2), (2, 4), (4, 6), (6, 7), (7, 8)]
        later_psi = {0: [4, 5], 1: [6, 7]}
        kbs = [work.tile([P, G, 2 * P, 4], BF16, align_bytes=64, bufs=5, name="kb") for i in groups]

        on_vector = (4,)

        def first(i):
            n0, n1 = groups[i]
            if i in on_vector:
                nc.vector.tensor_tensor(
                    out=fours(kbs[i][:, 0, 0 : P * (n1 - n0), :]),
                    in0=slots(psi[:, :, P * n0 : P * n1]),
                    in1=vv[:, 0:1, 0:4].unsqueeze(3).to_broadcast([P, 32 * (n1 - n0), 4, 4]),
                    op=ALU.mult,
                )
            else:
                first_block(n0, n1, scaled_psi(n0, n1), kbs[i])

        first(0)
        slopes_0(0, 2)
        for i in range(3):
            n0, n1 = groups[i]
            second_block(n0, n1, kbs[i])
            slopes_0(*groups[i + 1])
            if i == 0:
                w_quant(2)
                w_quant(3)
            else:
                quant_pair(groups[i - 1][0], kbs[i - 1])
            if i == 0:
                make_slopes(2, 4, 8)
            for nt in later_psi.get(i, ()):
                make_psi(nt)
            first(i + 1)
            for c in range(2):
                other_block(n0, n1, c, kbs[i])
            if i > 0:
                for nt in range(*groups[i - 1]):
                    stage2(nt)
        join_out(0, nc.scalar.copy, slice(0, S))
        second_block(6, 7, kbs[3])
        slopes_0(7, 8)
        quant_pair(4, kbs[2])
        first(4)
        other_block(6, 7, 0, kbs[3])
        stage2(4)
        stage2(5)
        quant_block(6, 0, kbs[3])
        quant_block(6, 1, kbs[3])
        other_block(6, 7, 1, kbs[3])
        quant_block(6, 2, kbs[3])
        second_block(7, 8, kbs[4])
        quant_block(6, 3, kbs[3])
        stage2(6)
        quant_out(0, slice(0, S), nc.sync)
        store_scales(0, (nc.sync, nc.sync))
        other_block(7, 8, 0, kbs[4])
        quant_block(7, 0, kbs[4])
        quant_block(7, 1, kbs[4])
        other_block(7, 8, 1, kbs[4])
        quant_block(7, 2, kbs[4])
        quant_block(7, 3, kbs[4])
        ends = [psum.tile([P, S // 2], F32, tag="p", name="o_end") for h in range(2)]
        for g in range(G):
            for h in range(2):
                stage2_pass(ends[h][:], 7, g, slice(256 * h, 256 * h + 256), g == 0, g == G - 1)
        for h, copy in ((0, nc.vector.tensor_copy), (1, nc.scalar.copy)):
            cols = slice(256 * h, 256 * h + 256)
            copy(out=of[:, 1, 3, cols], in_=ends[h][:])
            nc.sync.dma_start(out=out_rows[1, 3][:, cols], in_=of[:, 1, 3, cols])
        join_out(1, nc.vector.tensor_copy, slice(0, 256))
        join_out(1, nc.scalar.copy, slice(320, S))
        join_out(1, nc.vector.tensor_copy, slice(256, 320))
        quant_out(1, slice(0, 256), nc.sync)
        quant_out(1, slice(256, S), nc.sync)
        store_scales(1, (nc.sync, nc.sync))
